import numpy as np
import ml_dtypes


def mxq(x, axis, fmt="e4m3"):
    dtype, down = {"e4m3": (ml_dtypes.float8_e4m3fn, 7), "e5m2": (ml_dtypes.float8_e5m2, 14)}[fmt]
    v = np.moveaxis(np.asarray(x, np.float32).astype(ml_dtypes.bfloat16).astype(np.float64), axis, -1)
    blocks = v.reshape(v.shape[:-1] + (-1, 32))
    amax = np.abs(blocks).max(-1, keepdims=True)
    byte = np.maximum(np.where(amax > 0, np.frexp(amax)[1] - 1 + 127, 0) - down, 1)
    scale = np.exp2(byte - 127.0)
    codes = (blocks / scale).astype(np.float32).astype(dtype).astype(np.float64)
    return np.moveaxis((codes * scale).reshape(v.shape), -1, axis)


WIDE = False


def mx_kscale(k):
    if not WIDE:
        return np.ones(k)
    levels = np.array([30, -30])
    if k % 512:
        return np.exp2(np.random.permutation(np.resize(levels, k // 32))).repeat(32)
    a = np.empty((k // 512, 16))
    for p in range(k // 512):
        a[p, :8] = np.random.permutation(np.resize(levels, 8))
        for g in range(8):
            far = levels[np.abs(levels - a[p, g]) >= 10]
            a[p, g + 8] = far[np.random.randint(len(far))]
    return np.exp2(a.ravel()).repeat(32)


BF16 = ml_dtypes.bfloat16


def bf(x):
    return np.asarray(x, np.float32).astype(BF16)


def f64(x):
    return np.asarray(x).astype(np.float64)


E2M1 = np.array([0.0, 0.5, 1.0, 1.5, 2.0, 3.0, 4.0, 6.0, -0.0, -0.5, -1.0, -1.5, -2.0, -3.0, -4.0, -6.0])


def pack_weight(w, fmt):
    k, n = w.shape
    w = f64(bf(w)).reshape(k // 32, 32, n)
    amax = np.abs(w).max(1)
    if fmt in ("e4m3", "e5m2"):
        byte = np.frexp(amax)[1] - 1 + 127 - (7 if fmt == "e4m3" else 14)
    else:
        mant, ex = np.frexp(amax / 6.0)
        byte = np.where(mant > 0.5, ex, ex - 1) + 127
    byte = np.clip(np.where(amax > 0, byte, 1), 1, 254)
    scaled = (w * np.exp2(127.0 - byte)[:, None, :]).reshape(k, n).astype(np.float32)
    by_word = np.ascontiguousarray(scaled.reshape(k // 512, 128, 4, n).transpose(0, 1, 3, 2))
    if fmt in ("e4m3", "e5m2"):
        words = by_word.astype(ml_dtypes.float8_e4m3fn if fmt == "e4m3" else ml_dtypes.float8_e5m2).view(np.uint8)
    else:
        c = by_word.astype(ml_dtypes.float4_e2m1fn).view(np.uint8) & 0xF
        words = c[..., 0::2] | (c[..., 1::2] << 4)
    return np.ascontiguousarray(words), np.ascontiguousarray(byte.astype(np.uint8).reshape(k // 512, 16, n))


def unpack_weight(words, scales, fmt):
    g, p, n, _ = words.shape
    if fmt in ("e4m3", "e5m2"):
        vals = np.ascontiguousarray(words).view(ml_dtypes.float8_e4m3fn if fmt == "e4m3" else ml_dtypes.float8_e5m2).astype(np.float64)
    else:
        nib = np.empty((g, p, n, 4), np.uint8)
        nib[..., 0::2] = words & 0xF
        nib[..., 1::2] = words >> 4
        vals = E2M1[nib]
    vals = vals * np.repeat(np.exp2(scales.astype(np.float64) - 127.0), 8, axis=1)[..., None]
    return vals.transpose(0, 1, 3, 2).reshape(g * 512, n)

def planes(Y):
    n, m = Y.shape
    b = f64(bf(Y)).reshape(n // 32, 32, m)
    amax = np.abs(b).max(1)
    byte = np.clip(np.where(amax > 0, np.frexp(amax)[1] - 1 + 127 - 7, 1), 1, 254)
    codes = (b * np.exp2(127.0 - byte)[:, None, :]).reshape(n, m).astype(np.float32).astype(ml_dtypes.float8_e4m3fn).view(np.uint8)
    words = codes.reshape(n // 512, 128, 4, m).transpose(0, 1, 3, 2)
    return np.ascontiguousarray(words), np.ascontiguousarray(byte.astype(np.uint8).reshape(n // 512, 16, m))


R, C, T = 2048, 1024, 1536

PEAK = 2.0
SPREAD = 0.8
TAIL = 4.0

def soft_rows(logits):
    e = np.exp(logits - logits.max(axis=1, keepdims=True))
    return e / e.sum(axis=1, keepdims=True)

def setup_inputs():
    s = mx_kscale(R)
    logits = PEAK * np.random.randn(R, C) + SPREAD * np.random.randn(C)
    z = soft_rows(logits)
    d = 3.0 * np.random.standard_t(TAIL, size=(R, T))
    target_words, target_scales = pack_weight(d / s[:, None], "e5m2")
    prior = np.exp(SPREAD * np.random.randn(C, 1)) * np.random.randn(C, T)
    return {
        "member": bf(z * s[:, None]),
        "target_words": target_words,
        "target_scales": target_scales,
        "counts": bf(z.sum(axis=0)),
        "smooth": bf(np.exp(0.5 * np.random.randn(T))),
        "prior": bf(prior),
    }

def reference(member, target_words, target_scales, counts, smooth, prior):
    D = unpack_weight(target_words, target_scales, "e5m2")
    Zq = mxq(f64(member), 0, "e4m3")
    S = Zq.T @ D
    top = S + f64(smooth) * f64(prior)
    y = top / (f64(counts)[:, None] + f64(smooth))
    Y = y.reshape(C, T)
    words, scales = planes(Y)
    return y, words, scales

@@ -1,0 +1,442 @@
+from contextlib import ExitStack
+
+import concourse.mybir as mybir
+from concourse.masks import make_identity
+
+R, C, T = 2048, 1024, 1536
+FLOPS = 2 * R * C * T
+
+F32 = mybir.dt.float32
+BF16 = mybir.dt.bfloat16
+U32 = mybir.dt.uint32
+I32 = mybir.dt.int32
+U8 = mybir.dt.uint8
+E4M3X4 = mybir.dt.float8_e4m3fn_x4
+E5M2X4 = mybir.dt.float8_e5m2_x4
+ACT = mybir.ActivationFunctionType
+ALU = mybir.AluOpType
+
+P = 128
+PACK = 4
+W = 512
+HALF = W // 2
+PASSES = R // W
+GROUPS = C // W
+BLOCKS = T // W
+STRIPS = T // P
+HEAD_BLOCKS = 2
+HEAD_ROUNDS = 2 * HEAD_BLOCKS
+WR = [0, 0, 0, 2, 2, 2, 2, 2, 2]
+MP = {1: 1, 2: 2, 4: 3}
+AS = [3]
+HV = [0, 1]
+
+
+def tile_smoothed_target_encoding_k2_kernel(
+    tc, member, target_words, target_scales, counts, smooth, prior, out_0, out_1, out_2
+):
+    nc = tc.nc
+
+    with ExitStack() as ctx:
+        keep = ctx.enter_context(tc.tile_pool(name="keep", bufs=1))
+        ring = ctx.enter_context(tc.tile_pool(name="ring", bufs=3))
+        psum = ctx.enter_context(tc.psum_pool(name="psum", bufs=8))
+        ctx.enter_context(tc.manual_schedule())
+
+        def bank():
+            return psum.tile([P, W], F32, name="bank")
+
+        def rows_of_group(tensor, g, col0, width):
+            return tensor[g * W : (g + 1) * W, col0 : col0 + width].rearrange("(p t) c -> p t c", t=PACK)
+
+        smooth_rows = keep.tile([P, P], BF16, name="smooth_rows")
+        nc.vector.memset(smooth_rows[:], 0.0)
+        d_scales = keep.tile([P, PASSES, T], U8, name="d_scales", align_bytes=64)
+        nc.vector.memset(d_scales[:].bitcast(I32), 0)
+        warm = keep.tile([P, 1], F32, name="warm")
+        nc.vector.memset(warm[:], 1.0)
+
+        count_bf = keep.tile([P, GROUPS, PACK], BF16, name="count_bf")
+        nc.scalar.dma_start(out=count_bf[:], in_=counts.rearrange("(g p t) -> p g t", g=GROUPS, t=PACK))
+        nc.scalar.dma_start(out=smooth_rows[0:STRIPS, :], in_=smooth.rearrange("(b j) -> b j", j=P))
+        warm_out = keep.tile([P, 1], F32, name="warm_out")
+        nc.scalar.activation(out=warm_out[:], in_=warm[:], func=ACT.Ln)
+
+        ident_bf = keep.tile([P, P], BF16, name="ident_bf")
+        make_identity(nc, ident_bf[:])
+        ident_f32 = keep.tile([P, P], F32, name="ident_f32")
+        make_identity(nc, ident_f32[:])
+
+        member_raw = {}
+        d_head = {}
+        prior_sb = {}
+
+        def load_member(g, k):
+            member_raw[g, k] = keep.tile([P, PACK, W], BF16, name="member_raw_%d_%d" % (g, k))
+            nc.sync.dma_start(out=member_raw[g, k][:], in_=rows_of_group(member, k, g * W, W))
+
+        def load_prior(g, b):
+            prior_sb[g, b] = keep.tile([P, PACK, W], BF16, name="prior_%d_%d" % (g, b))
+            nc.sync.dma_start(out=prior_sb[g, b][:], in_=rows_of_group(prior, g, b * W, W))
+
+        d_words = target_words.rearrange("k p n t -> p k (n t)").bitcast(I32)
+        head_w = HEAD_BLOCKS * W
+        def load_d_head(k):
+            d_head[k] = keep.tile([P, head_w], U32, name="d_head_%d" % k, align_bytes=64)
+            nc.sync.dma_start(out=d_head[k][:].bitcast(I32), in_=d_words[:, k, 0:head_w])
+
+        load_member(0, 0)
+        for q in range(4):
+            nc.sync.dma_start(
+                out=d_scales[32 * q : 32 * q + 4, :, :].bitcast(I32),
+                in_=target_scales[:, 4 * q : 4 * q + 4, :].rearrange("k r n -> r k n").bitcast(I32),
+            )
+        load_d_head(0)
+        load_member(0, 1)
+        load_member(0, 2)
+        load_d_head(1)
+        load_member(0, 3)
+        load_d_head(2)
+        load_member(1, 0)
+        load_d_head(3)
+        d_rest = {}
+
+        def load_d_block(b):
+            d_rest[b] = keep.tile([P, PASSES, W], U32, name="d_block_%d" % b, align_bytes=64)
+            nc.sync.dma_start(out=d_rest[b][:].bitcast(I32), in_=d_words[:, :, b * W : (b + 1) * W])
+
+        load_prior(0, 0)
+        load_member(1, 1)
+        load_prior(0, 1)
+        load_member(1, 2)
+        load_d_block(2)
+        load_member(1, 3)
+        load_prior(0, 2)
+        for b in range(BLOCKS):
+            load_prior(1, b)
+
+        def d_codes(k, col0, width):
+            if col0 < head_w:
+                return d_head[k][:, col0 : col0 + width].bitcast(E5M2X4)
+            return d_rest[col0 // W][:, k, col0 % W : col0 % W + width].bitcast(E5M2X4)
+
+        ln_smooth = keep.tile([P, T], F32, name="ln_smooth")
+        spread = [bank() for b in range(BLOCKS)]
+        for s in range(STRIPS):
+            nc.tensor.matmul(
+                out=spread[s // PACK][:, (s % PACK) * P : (s % PACK + 1) * P],
+                lhsT=ident_bf[:, s : s + 1].to_broadcast([P, P]),
+                rhs=smooth_rows[:],
+                start=True,
+                stop=True,
+            )
+        turned = bank()
+        nc.tensor.matmul(out=turned[:, 0:16], lhsT=smooth_rows[:], rhs=ident_bf[:, 0:16], start=True, stop=True)
+        inv_smooth = keep.tile([P, STRIPS], F32, name="inv_smooth")
+        count_cols = count_bf[:].rearrange("p g t -> p (g t)")
+        inv_count = keep.tile([P, GROUPS * PACK], F32, name="inv_count")
+        ln_count = keep.tile([P, GROUPS * PACK], F32, name="ln_count")
+        nc.scalar.activation(out=ln_count[:], in_=count_cols, func=ACT.Ln)
+        for b in range(BLOCKS):
+            nc.scalar.activation(out=ln_smooth[:, b * W : (b + 1) * W], in_=spread[b][:], func=ACT.Ln)
+        neg_ln_count = keep.tile([P, GROUPS * PACK], F32, name="neg_ln_count")
+
+        member_codes = {}
+        member_scales = {}
+        grouped = {}
+
+        def interleave(g, k, h, engine):
+            tile = ring.tile([P, HALF, PACK], BF16, name="grouped", bufs=4, align_bytes=64)
+            grouped[g, k, h] = tile
+            raw = member_raw[g, k]
+            src = raw[:].rearrange("p j (m e t) -> p m t e j", e=2, t=PACK)[:, :, 2 * h : 2 * h + 2]
+            dst = tile[:].rearrange("p (t m e) j -> p m t e j", t=2, e=2)
+            if engine == "vector":
+                nc.vector.tensor_copy(out=dst, in_=src)
+            else:
+                nc.scalar.copy(out=dst, in_=src)
+
+        def quantise_member(g, k, h):
+            if h == 0:
+                member_codes[g, k] = keep.tile([P, W], U32, name="member_codes_%d_%d" % (g, k), align_bytes=64)
+                member_scales[g, k] = keep.tile([P, W], U8, name="member_scales_%d_%d" % (g, k), align_bytes=64)
+            cols = slice(h * HALF, (h + 1) * HALF)
+            nc.vector.quantize_mx(
+                out=member_codes[g, k][:, cols].bitcast(E4M3X4),
+                scales=member_scales[g, k][:, cols],
+                in_=grouped[g, k, h][:].rearrange("p c j -> p (c j)"),
+            )
+
+        turned_blocks = [(0, 0), (0, 1), (0, 2), (1, 1), (1, 2)]
+        weight = {}
+
+        def make_weight(g, b, t):
+            if t == 0:
+                weight[g, b] = ring.tile([P, PACK, W], F32, name="weight", bufs=4)
+            col = g * PACK + t
+            if (g, b) in turned_blocks:
+                bias, scale = neg_ln_count[:, col : col + 1], 1.0
+            else:
+                bias, scale = ln_count[:, col : col + 1], -1.0
+            nc.scalar.activation(
+                out=weight[g, b][:, t, :], in_=ln_smooth[:, b * W : (b + 1) * W], func=ACT.Sigmoid, bias=bias, scale=scale
+            )
+
+        weights_due = [(g, b, t) for g, b in [(0, 0), (0, 1), (0, 2), (1, 0), (1, 1), (1, 2)] for t in range(PACK)]
+
+        def make_weights(n):
+            for piece in weights_due[:n]:
+                make_weight(*piece)
+                weights_due.remove(piece)
+
+        sums = {}
+        scaled = {}
+        joined = {}
+        y_tile = {}
+        shrunk_prior = {}
+        y_bf = {}
+        y_codes = [keep.tile([P, T], U32, name="y_codes_%d" % g, align_bytes=64) for g in range(GROUPS)]
+        y_scales = [keep.tile([P, T], U8, name="y_scales_%d" % g, align_bytes=64) for g in range(GROUPS)]
+
+        def mx_pass(unit, k):
+            g, b, i = unit
+            if k == 0:
+                sums[unit] = bank()
+            if (g, b) in turned_blocks:
+                col0 = b * W + i * P
+                nc.tensor.matmul_mx(
+                    out=sums[unit][:],
+                    lhsT=d_codes(k, col0, P),
+                    lhsT_scale=d_scales[:, k, col0 : col0 + P],
+                    rhs=member_codes[g, k][:].bitcast(E4M3X4),
+                    rhs_scale=member_scales[g, k][:],
+                    start=(k == 0),
+                    stop=(k == PASSES - 1),
+                )
+            else:
+                nc.tensor.matmul_mx(
+                    out=sums[unit][:],
+                    lhsT=member_codes[g, k][:, i * P : (i + 1) * P].bitcast(E4M3X4),
+                    lhsT_scale=member_scales[g, k][:, i * P : (i + 1) * P],
+                    rhs=d_codes(k, b * W, W),
+                    rhs_scale=d_scales[:, k, b * W : (b + 1) * W],
+                    start=(k == 0),
+                    stop=(k == PASSES - 1),
+                )
+
+        def scale_out(unit):
+            g, b, i = unit
+            scaled[unit] = ring.tile([P, PACK, P], F32, name="scaled", bufs=4)
+            src = sums[unit][:].rearrange("p (t m) -> p t m", t=PACK)
+            strip = b * PACK + i
+            nc.scalar.activation(out=scaled[unit][:], in_=src, func=ACT.Copy, scale=inv_smooth[:, strip : strip + 1])
+
+        def lay_prior(unit):
+            g, b, i = unit
+            joined[unit] = bank()
+            nc.tensor.matmul(
+                out=joined[unit][:].rearrange("p (t j) -> p t j", t=PACK),
+                lhsT=ident_bf[:],
+                rhs=prior_sb[g, b][:, :, i * P : (i + 1) * P],
+                start=True,
+                stop=False,
+            )
+
+        def turn_and_add(unit):
+            for t in range(PACK):
+                nc.tensor.matmul(
+                    out=joined[unit][:, t * P : (t + 1) * P],
+                    lhsT=scaled[unit][:, t, :],
+                    rhs=ident_f32[:],
+                    is_transpose=True,
+                    start=False,
+                    stop=(t == PACK - 1),
+                )
+
+        def weigh(unit):
+            g, b, i = unit
+            if i % 2 == 0:
+                y_tile[g, b, i // 2] = ring.tile([P, PACK, HALF], F32, name="y_half", bufs=6)
+            c0 = (i % 2) * P
+            nc.vector.tensor_tensor(
+                out=y_tile[g, b, i // 2][:, :, c0 : c0 + P],
+                in0=joined[unit][:].rearrange("p (t j) -> p t j", t=PACK),
+                in1=weight[g, b][:, :, i * P : (i + 1) * P],
+                op=ALU.mult,
+            )
+
+        def shrink_prior(unit):
+            g, b, t = unit
+            shrunk_prior[unit] = ring.tile([P, W], F32, name="shrunk_prior", bufs=4)
+            nc.vector.scalar_tensor_tensor(
+                out=shrunk_prior[unit][:],
+                in0=weight[g, b][:, t, :],
+                scalar=1.0,
+                in1=prior_sb[g, b][:, t, :],
+                op0=ALU.subtract,
+                op1=ALU.mult,
+            )
+
+        def weigh_sums(unit):
+            g, b, t = unit
+            if t == 0:
+                y_tile[g, b] = ring.tile([P, PACK, W], F32, name="y_block", bufs=2)
+            col = g * PACK + t
+            nc.vector.scalar_tensor_tensor(
+                out=y_tile[g, b][:, t, :],
+                in0=sums[unit][:],
+                scalar=inv_count[:, col : col + 1],
+                in1=weight[g, b][:, t, :],
+                op0=ALU.mult,
+                op1=ALU.mult,
+            )
+
+        def join_prior(unit):
+            g, b, t = unit
+            row = y_tile[g, b][:, t, :]
+            nc.vector.tensor_tensor(out=row, in0=row, in1=shrunk_prior[unit][:], op=ALU.subtract)
+
+        def round_y(g, col0, width, source, engine):
+            tile = ring.tile([P, HALF, PACK], BF16, name="y_bf", bufs=4, align_bytes=64)
+            y_bf[g, col0] = tile
+            src = source.rearrange("p t (c i) -> p c t i", i=2)
+            dst = tile[:, 0:width, :].rearrange("p (c i) t -> p c t i", i=2)
+            if engine == "vector":
+                nc.vector.tensor_copy(out=dst, in_=src)
+            else:
+                nc.scalar.copy(out=dst, in_=src)
+
+        def quantise_y(g, col0, width):
+            nc.vector.quantize_mx(
+                out=y_codes[g][:, col0 : col0 + width].bitcast(E4M3X4),
+                scales=y_scales[g][:, col0 : col0 + width],
+                in_=y_bf[g, col0][:, 0:width, :].rearrange("p c t -> p (c t)"),
+            )
+
+        def store_codes(g, col0, width):
+            words = out_1[g].rearrange("p m t -> p (m t)").bitcast(I32)
+            nc.sync.dma_start(out=words[:, col0 : col0 + width], in_=y_codes[g][:, col0 : col0 + width].bitcast(I32))
+
+        def store_scales(g, col0, width, queues):
+            for q in range(4):
+                queues[q % len(queues)].dma_start(
+                    out=out_2[g, 4 * q : 4 * q + 4, col0 : col0 + width].bitcast(I32),
+                    in_=y_scales[g][32 * q : 32 * q + 4, col0 : col0 + width].bitcast(I32),
+                )
+
+        def pair(g, b, h):
+            return [(g, b, 2 * h), (g, b, 2 * h + 1)]
+
+        rounds = [pair(g, b, h) for g in range(GROUPS) for b in range(BLOCKS) for h in range(2)]
+
+        def is_turned(r):
+            return 0 <= r < len(rounds) and rounds[r][0][:2] in turned_blocks
+
+        def is_plain(r):
+            return 0 <= r < len(rounds) and not is_turned(r)
+
+        for k in range(PASSES):
+            interleave(0, k, 0, "vector")
+            interleave(0, k, 1, "vector")
+            quantise_member(0, k, 0)
+            quantise_member(0, k, 1)
+            if k == 0:
+                nc.vector.reciprocal(out=inv_smooth[:], in_=turned[:, 0:STRIPS])
+                nc.vector.reciprocal(out=inv_count[:], in_=count_cols)
+                nc.vector.tensor_scalar(out=neg_ln_count[:], in0=ln_count[:], scalar1=-1.0, scalar2=None, op0=ALU.mult)
+            if k < PASSES - 1:
+                for r in range(HEAD_ROUNDS):
+                    for unit in rounds[r]:
+                        mx_pass(unit, k)
+        interleave(1, 0, 0, "vector")
+        interleave(1, 0, 1, "vector")
+        quantise_member(1, 0, 0)
+        quantise_member(1, 0, 1)
+        make_weights(12)
+        weights_in_round = WR
+
+        last = len(rounds) - 1
+
+        def halves_done(r):
+            if not 0 <= r <= last:
+                return []
+            g, b, i = rounds[r][0]
+            if is_turned(r):
+                return [(g, b * W + i * P, y_tile[g, b, i // 2][:])]
+            if i == 2:
+                return [(g, b * W + h * HALF, y_tile[g, b][:, :, h * HALF : (h + 1) * HALF]) for h in range(2)]
+            return []
+
+        def finish(r):
+            for g, col0, y in halves_done(r):
+                quantise_y(g, col0, HALF)
+                if col0 % W:
+                    store_codes(g, col0 - HALF, W)
+                if col0 == T - HALF:
+                    store_scales(g, 0, T, [nc.sync] if g == 0 else [nc.scalar, nc.sync])
+
+        for r in range(len(rounds) + 1):
+            if r <= last:
+                for unit in rounds[r]:
+                    for k in range(PASSES - 1 if r < HEAD_ROUNDS else 0, PASSES):
+                        mx_pass(unit, k)
+            n_weights = weights_in_round[r] if r < len(weights_in_round) else 0
+            member_pass = MP.get(r)
+            on_vector = r - 2 in HV
+            if member_pass in AS:
+                interleave(1, member_pass, 1, "scalar")
+            if is_turned(r):
+                scale_out(rounds[r][0])
+            make_weights(n_weights // 2)
+            if is_turned(r):
+                scale_out(rounds[r][1])
+            make_weights(n_weights - n_weights // 2)
+            if not on_vector:
+                for g, col0, y in halves_done(r - 2):
+                    round_y(g, col0, HALF, y, "scalar")
+            if is_turned(r - 1):
+                for unit in rounds[r - 1]:
+                    lay_prior(unit)
+                for unit in rounds[r - 1]:
+                    turn_and_add(unit)
+            if on_vector:
+                for g, col0, y in halves_done(r - 2):
+                    round_y(g, col0, HALF, y, "vector")
+            if member_pass is not None:
+                interleave(1, member_pass, 0, "vector")
+                if member_pass not in AS:
+                    interleave(1, member_pass, 1, "vector")
+            if on_vector:
+                finish(r - 2)
+            if member_pass is not None:
+                quantise_member(1, member_pass, 0)
+                quantise_member(1, member_pass, 1)
+            if is_plain(r):
+                weigh_sums(rounds[r][0])
+                weigh_sums(rounds[r][1])
+            if is_turned(r - 1) and is_plain(r):
+                weigh(rounds[r - 1][0])
+                weigh(rounds[r - 1][1])
+            if is_plain(r):
+                shrink_prior(rounds[r][0])
+                shrink_prior(rounds[r][1])
+                join_prior(rounds[r][0])
+                join_prior(rounds[r][1])
+            if r - 3 not in HV:
+                finish(r - 3)
+            if is_turned(r - 1) and not is_plain(r):
+                weigh(rounds[r - 1][0])
+                weigh(rounds[r - 1][1])
+            if is_turned(r - 1):
+                g, col0, y = halves_done(r - 1)[0]
+                nc.sync.dma_start(out=rows_of_group(out_0, g, col0, HALF), in_=y)
+            if is_plain(r):
+                g, b, i = rounds[r][0]
+                nc.sync.dma_start(
+                    out=rows_of_group(out_0, g, b * W, W)[:, i : i + 2, :], in_=y_tile[g, b][:, i : i + 2, :]
+                )
+        g, col0, y = halves_done(last)[0]
+        round_y(g, col0, HALF, y, "vector")
+        if last - 1 not in HV:
+            finish(last - 1)
+        finish(last)

@@ -26,10 +26,9 @@ BLOCKS = T // W
 STRIPS = T // P
 HEAD_BLOCKS = 2
 HEAD_ROUNDS = 2 * HEAD_BLOCKS
-WR = [0, 0, 0, 2, 2, 2, 2, 2, 2]
-MP = {1: 1, 2: 2, 4: 3}
-AS = [3]
-HV = [0, 1]
+MP = {0: 0, 2: 1, 4: 2, 5: 3}
+HV = [8, 9]
+JOBS = {3: [("w", 1, 0, 0)], 4: [("H", 0, 0), ("w", 1, 0, 2)], 5: [("H", 1, 0), ("W", 0)], 6: [("W", 1), ("W", 2), ("H", 2, 0)], 7: [("W", 3), ("H", 3, 0), ("H", 4, 0)], 8: [("H", 5, 0)], 10: [("H", 7, 0), ("H", 7, 1)], 12: [("H", 10, 0)]}
 
 
 def tile_smoothed_target_encoding_k2_kernel(
@@ -58,7 +57,9 @@ def tile_smoothed_target_encoding_k2_kernel(
 
         count_bf = keep.tile([P, GROUPS, PACK], BF16, name="count_bf")
         nc.scalar.dma_start(out=count_bf[:], in_=counts.rearrange("(g p t) -> p g t", g=GROUPS, t=PACK))
-        nc.scalar.dma_start(out=smooth_rows[0:STRIPS, :], in_=smooth.rearrange("(b j) -> b j", j=P))
+        smooth_strips = smooth.rearrange("(b j) -> b j", j=P)
+        nc.scalar.dma_start(out=smooth_rows[0:8, :], in_=smooth_strips[0:8, :])
+        nc.scalar.dma_start(out=smooth_rows[8:STRIPS, :], in_=smooth_strips[8:STRIPS, :])
         warm_out = keep.tile([P, 1], F32, name="warm_out")
         nc.scalar.activation(out=warm_out[:], in_=warm[:], func=ACT.Ln)
 
@@ -85,20 +86,19 @@ def tile_smoothed_target_encoding_k2_kernel(
             d_head[k] = keep.tile([P, head_w], U32, name="d_head_%d" % k, align_bytes=64)
             nc.sync.dma_start(out=d_head[k][:].bitcast(I32), in_=d_words[:, k, 0:head_w])
 
+        def load_d_scales(col0, width):
+            for q in range(4):
+                nc.sync.dma_start(
+                    out=d_scales[32 * q : 32 * q + 4, :, col0 : col0 + width].bitcast(I32),
+                    in_=target_scales[:, 4 * q : 4 * q + 4, col0 : col0 + width].rearrange("k r n -> r k n").bitcast(I32),
+                )
+
         load_member(0, 0)
-        for q in range(4):
-            nc.sync.dma_start(
-                out=d_scales[32 * q : 32 * q + 4, :, :].bitcast(I32),
-                in_=target_scales[:, 4 * q : 4 * q + 4, :].rearrange("k r n -> r k n").bitcast(I32),
-            )
+        load_d_scales(0, head_w)
         load_d_head(0)
-        load_member(0, 1)
-        load_member(0, 2)
-        load_d_head(1)
-        load_member(0, 3)
-        load_d_head(2)
-        load_member(1, 0)
-        load_d_head(3)
+        for k in range(1, PASSES):
+            load_member(0, k)
+            load_d_head(k)
         d_rest = {}
 
         def load_d_block(b):
@@ -106,10 +106,12 @@ def tile_smoothed_target_encoding_k2_kernel(
             nc.sync.dma_start(out=d_rest[b][:].bitcast(I32), in_=d_words[:, :, b * W : (b + 1) * W])
 
         load_prior(0, 0)
-        load_member(1, 1)
+        load_member(1, 0)
         load_prior(0, 1)
-        load_member(1, 2)
+        load_member(1, 1)
+        load_d_scales(head_w, T - head_w)
         load_d_block(2)
+        load_member(1, 2)
         load_member(1, 3)
         load_prior(0, 2)
         for b in range(BLOCKS):
@@ -146,21 +148,21 @@ def tile_smoothed_target_encoding_k2_kernel(
         grouped = {}
 
         def interleave(g, k, h, engine):
-            tile = ring.tile([P, HALF, PACK], BF16, name="grouped", bufs=4, align_bytes=64)
-            grouped[g, k, h] = tile
-            raw = member_raw[g, k]
-            src = raw[:].rearrange("p j (m e t) -> p m t e j", e=2, t=PACK)[:, :, 2 * h : 2 * h + 2]
-            dst = tile[:].rearrange("p (t m e) j -> p m t e j", t=2, e=2)
-            if engine == "vector":
-                nc.vector.tensor_copy(out=dst, in_=src)
+            if g == 0:
+                grouped[g, k, h] = ring.tile([P, HALF, PACK], BF16, name="grouped_half", bufs=2, align_bytes=64)
+                src = member_raw[g, k][:, :, h * HALF : (h + 1) * HALF].rearrange("p j (c i) -> p c j i", i=4)
+                dst = grouped[g, k, h][:].rearrange("p (c i) j -> p c j i", i=4)
             else:
-                nc.scalar.copy(out=dst, in_=src)
+                grouped[g, k, h] = ring.tile([P, W, PACK], BF16, name="grouped", bufs=2, align_bytes=64)
+                src = member_raw[g, k][:].rearrange("p j (m e t) -> p m t e j", e=2, t=PACK)
+                dst = grouped[g, k, h][:].rearrange("p (t m e) j -> p m t e j", t=PACK, e=2)
+            nc.vector.tensor_copy(out=dst, in_=src)
 
         def quantise_member(g, k, h):
-            if h == 0:
+            if (g, k) not in member_codes:
                 member_codes[g, k] = keep.tile([P, W], U32, name="member_codes_%d_%d" % (g, k), align_bytes=64)
                 member_scales[g, k] = keep.tile([P, W], U8, name="member_scales_%d_%d" % (g, k), align_bytes=64)
-            cols = slice(h * HALF, (h + 1) * HALF)
+            cols = slice(0, W) if h is None else slice(h * HALF, (h + 1) * HALF)
             nc.vector.quantize_mx(
                 out=member_codes[g, k][:, cols].bitcast(E4M3X4),
                 scales=member_scales[g, k][:, cols],
@@ -170,24 +172,24 @@ def tile_smoothed_target_encoding_k2_kernel(
         turned_blocks = [(0, 0), (0, 1), (0, 2), (1, 1), (1, 2)]
         weight = {}
 
-        def make_weight(g, b, t):
+        def make_weight(g, b, t, blocks):
             if t == 0:
-                weight[g, b] = ring.tile([P, PACK, W], F32, name="weight", bufs=4)
+                tile = ring.tile([P, PACK, blocks * W], F32, name="weight_%d" % blocks, bufs=2 // blocks)
+                for extra in range(blocks):
+                    weight[g, b + extra] = tile[:, :, extra * W : (extra + 1) * W]
+                weight[g, b, blocks] = tile
             col = g * PACK + t
             if (g, b) in turned_blocks:
                 bias, scale = neg_ln_count[:, col : col + 1], 1.0
             else:
                 bias, scale = ln_count[:, col : col + 1], -1.0
             nc.scalar.activation(
-                out=weight[g, b][:, t, :], in_=ln_smooth[:, b * W : (b + 1) * W], func=ACT.Sigmoid, bias=bias, scale=scale
+                out=weight[g, b, blocks][:, t, :],
+                in_=ln_smooth[:, b * W : (b + blocks) * W],
+                func=ACT.Sigmoid,
+                bias=bias,
+                scale=scale,
             )
-
-        weights_due = [(g, b, t) for g, b in [(0, 0), (0, 1), (0, 2), (1, 0), (1, 1), (1, 2)] for t in range(PACK)]
-
-        def make_weights(n):
-            for piece in weights_due[:n]:
-                make_weight(*piece)
-                weights_due.remove(piece)
 
         sums = {}
         scaled = {}
@@ -227,7 +229,10 @@ def tile_smoothed_target_encoding_k2_kernel(
         def scale_out(unit):
             g, b, i = unit
             scaled[unit] = ring.tile([P, PACK, P], F32, name="scaled", bufs=4)
-            src = sums[unit][:].rearrange("p (t m) -> p t m", t=PACK)
+            if g == 0:
+                src = sums[unit][:].rearrange("p (m t) -> p t m", t=PACK)
+            else:
+                src = sums[unit][:].rearrange("p (t m) -> p t m", t=PACK)
             strip = b * PACK + i
             nc.scalar.activation(out=scaled[unit][:], in_=src, func=ACT.Copy, scale=inv_smooth[:, strip : strip + 1])
 
@@ -267,7 +272,7 @@ def tile_smoothed_target_encoding_k2_kernel(
 
         def shrink_prior(unit):
             g, b, t = unit
-            shrunk_prior[unit] = ring.tile([P, W], F32, name="shrunk_prior", bufs=4)
+            shrunk_prior[unit] = ring.tile([P, W], F32, name="shrunk_prior", bufs=2)
             nc.vector.scalar_tensor_tensor(
                 out=shrunk_prior[unit][:],
                 in0=weight[g, b][:, t, :],
@@ -280,7 +285,7 @@ def tile_smoothed_target_encoding_k2_kernel(
         def weigh_sums(unit):
             g, b, t = unit
             if t == 0:
-                y_tile[g, b] = ring.tile([P, PACK, W], F32, name="y_block", bufs=2)
+                y_tile[g, b] = ring.tile([P, PACK, W], F32, name="y_block", bufs=1)
             col = g * PACK + t
             nc.vector.scalar_tensor_tensor(
                 out=y_tile[g, b][:, t, :],
@@ -297,10 +302,10 @@ def tile_smoothed_target_encoding_k2_kernel(
             nc.vector.tensor_tensor(out=row, in0=row, in1=shrunk_prior[unit][:], op=ALU.subtract)
 
         def round_y(g, col0, width, source, engine):
-            tile = ring.tile([P, HALF, PACK], BF16, name="y_bf", bufs=4, align_bytes=64)
+            tile = ring.tile([P, HALF, PACK], BF16, name="y_bf", bufs=5, align_bytes=64)
             y_bf[g, col0] = tile
-            src = source.rearrange("p t (c i) -> p c t i", i=2)
-            dst = tile[:, 0:width, :].rearrange("p (c i) t -> p c t i", i=2)
+            src = source.rearrange("p t (c i) -> p c t i", i=4)
+            dst = tile[:, 0:width, :].rearrange("p (c i) t -> p c t i", i=4)
             if engine == "vector":
                 nc.vector.tensor_copy(out=dst, in_=src)
             else:
@@ -336,107 +341,120 @@ def tile_smoothed_target_encoding_k2_kernel(
             return 0 <= r < len(rounds) and not is_turned(r)
 
         for k in range(PASSES):
-            interleave(0, k, 0, "vector")
-            interleave(0, k, 1, "vector")
-            quantise_member(0, k, 0)
-            quantise_member(0, k, 1)
+            for h in range(2):
+                interleave(0, k, h, "vector")
+            for h in range(2):
+                quantise_member(0, k, h)
             if k == 0:
+                nc.vector.tensor_scalar(out=neg_ln_count[:], in0=ln_count[:], scalar1=-1.0, scalar2=None, op0=ALU.mult)
                 nc.vector.reciprocal(out=inv_smooth[:], in_=turned[:, 0:STRIPS])
                 nc.vector.reciprocal(out=inv_count[:], in_=count_cols)
-                nc.vector.tensor_scalar(out=neg_ln_count[:], in0=ln_count[:], scalar1=-1.0, scalar2=None, op0=ALU.mult)
+                for t in range(PACK):
+                    make_weight(0, 0, t, 2)
+                for t in range(PACK):
+                    make_weight(0, 2, t, 1)
             if k < PASSES - 1:
                 for r in range(HEAD_ROUNDS):
                     for unit in rounds[r]:
                         mx_pass(unit, k)
-        interleave(1, 0, 0, "vector")
-        interleave(1, 0, 1, "vector")
-        quantise_member(1, 0, 0)
-        quantise_member(1, 0, 1)
-        make_weights(12)
-        weights_in_round = WR
 
         last = len(rounds) - 1
 
-        def halves_done(r):
-            if not 0 <= r <= last:
-                return []
+        def half(r, h=0):
             g, b, i = rounds[r][0]
             if is_turned(r):
-                return [(g, b * W + i * P, y_tile[g, b, i // 2][:])]
-            if i == 2:
-                return [(g, b * W + h * HALF, y_tile[g, b][:, :, h * HALF : (h + 1) * HALF]) for h in range(2)]
-            return []
+                return g, b * W + i * P, y_tile[g, b, i // 2][:]
+            return g, b * W + h * HALF, y_tile[g, b][:, :, h * HALF : (h + 1) * HALF]
 
-        def finish(r):
-            for g, col0, y in halves_done(r):
-                quantise_y(g, col0, HALF)
-                if col0 % W:
-                    store_codes(g, col0 - HALF, W)
-                if col0 == T - HALF:
-                    store_scales(g, 0, T, [nc.sync] if g == 0 else [nc.scalar, nc.sync])
+        def finish(r, h=0):
+            g, col0, y = half(r, h)
+            quantise_y(g, col0, HALF)
+            if col0 % W:
+                store_codes(g, col0 - HALF, W)
+            if (g, col0) == (0, T - HALF):
+                store_scales(g, 0, T, [nc.sync])
+
+        jobs = JOBS
+        rounded = []
+
+        def spare_job(job):
+            if job[0] == "w":
+                make_weight(job[1], job[2], job[3], 1)
+                make_weight(job[1], job[2], job[3] + 1, 1)
+            elif job[0] == "W":
+                make_weight(1, 1, job[1], 2)
+            else:
+                g, col0, y = half(job[1], job[2])
+                round_y(g, col0, HALF, y, "scalar")
+                rounded.append(job[1:])
 
         for r in range(len(rounds) + 1):
             if r <= last:
                 for unit in rounds[r]:
                     for k in range(PASSES - 1 if r < HEAD_ROUNDS else 0, PASSES):
                         mx_pass(unit, k)
-            n_weights = weights_in_round[r] if r < len(weights_in_round) else 0
             member_pass = MP.get(r)
             on_vector = r - 2 in HV
-            if member_pass in AS:
-                interleave(1, member_pass, 1, "scalar")
+            to_finish = list(rounded)
+            rounded.clear()
+            todo = jobs.get(r, [])
+            for job in todo[:1]:
+                spare_job(job)
             if is_turned(r):
                 scale_out(rounds[r][0])
-            make_weights(n_weights // 2)
+            for job in todo[1:2]:
+                spare_job(job)
             if is_turned(r):
                 scale_out(rounds[r][1])
-            make_weights(n_weights - n_weights // 2)
-            if not on_vector:
-                for g, col0, y in halves_done(r - 2):
-                    round_y(g, col0, HALF, y, "scalar")
+            for job in todo[2:]:
+                spare_job(job)
             if is_turned(r - 1):
                 for unit in rounds[r - 1]:
                     lay_prior(unit)
                 for unit in rounds[r - 1]:
                     turn_and_add(unit)
             if on_vector:
-                for g, col0, y in halves_done(r - 2):
-                    round_y(g, col0, HALF, y, "vector")
+                g, col0, y = half(r - 2)
+                round_y(g, col0, HALF, y, "vector")
             if member_pass is not None:
-                interleave(1, member_pass, 0, "vector")
-                if member_pass not in AS:
-                    interleave(1, member_pass, 1, "vector")
+                interleave(1, member_pass, None, "vector")
+            if r > last:
+                break
+            for done in to_finish:
+                finish(*done)
+            if member_pass is not None:
+                quantise_member(1, member_pass, None)
             if on_vector:
                 finish(r - 2)
-            if member_pass is not None:
-                quantise_member(1, member_pass, 0)
-                quantise_member(1, member_pass, 1)
             if is_plain(r):
                 weigh_sums(rounds[r][0])
                 weigh_sums(rounds[r][1])
-            if is_turned(r - 1) and is_plain(r):
+            if is_turned(r - 1):
                 weigh(rounds[r - 1][0])
                 weigh(rounds[r - 1][1])
+                g, col0, y = half(r - 1)
+                nc.sync.dma_start(out=rows_of_group(out_0, g, col0, HALF), in_=y)
             if is_plain(r):
                 shrink_prior(rounds[r][0])
                 shrink_prior(rounds[r][1])
                 join_prior(rounds[r][0])
                 join_prior(rounds[r][1])
-            if r - 3 not in HV:
-                finish(r - 3)
-            if is_turned(r - 1) and not is_plain(r):
-                weigh(rounds[r - 1][0])
-                weigh(rounds[r - 1][1])
-            if is_turned(r - 1):
-                g, col0, y = halves_done(r - 1)[0]
-                nc.sync.dma_start(out=rows_of_group(out_0, g, col0, HALF), in_=y)
-            if is_plain(r):
                 g, b, i = rounds[r][0]
                 nc.sync.dma_start(
                     out=rows_of_group(out_0, g, b * W, W)[:, i : i + 2, :], in_=y_tile[g, b][:, i : i + 2, :]
                 )
-        g, col0, y = halves_done(last)[0]
-        round_y(g, col0, HALF, y, "vector")
-        if last - 1 not in HV:
-            finish(last - 1)
-        finish(last)
+        for done in to_finish:
+            finish(*done)
+        store_scales(1, 0, T - W, [nc.sync])
+        weigh(rounds[last][0])
+        g, col0, y = half(last)
+        nc.sync.dma_start(out=rows_of_group(out_0, g, col0, P), in_=y[:, :, 0:P])
+        weigh(rounds[last][1])
+        nc.sync.dma_start(out=rows_of_group(out_0, g, col0 + P, P), in_=y[:, :, P:HALF])
+        round_y(g, col0, P, y[:, :, 0:P], "scalar")
+        round_y(g, col0 + P, P, y[:, :, P:HALF], "vector")
+        quantise_y(g, col0 - HALF, HALF)
+        quantise_y(g, col0, P)
+        quantise_y(g, col0 + P, P)
+        store_codes(g, col0 - HALF, W)
+        store_scales(g, T - W, W, [nc.scalar, nc.sync])

@@ -18,17 +18,19 @@ ALU = mybir.AluOpType
 
 P = 128
 PACK = 4
-W = 512
+W = P * PACK
 HALF = W // 2
 PASSES = R // W
 GROUPS = C // W
 BLOCKS = T // W
 STRIPS = T // P
+QUADRANTS = 4
+
+DIRECT_BLOCK = (1, 0)
 HEAD_BLOCKS = 2
-HEAD_ROUNDS = 2 * HEAD_BLOCKS
-MP = {0: 0, 2: 1, 4: 2, 5: 3}
-HV = [8, 9]
-JOBS = {3: [("w", 1, 0, 0)], 4: [("H", 0, 0), ("w", 1, 0, 2)], 5: [("H", 1, 0), ("W", 0)], 6: [("W", 1), ("W", 2), ("H", 2, 0)], 7: [("W", 3), ("H", 3, 0), ("H", 4, 0)], 8: [("H", 5, 0)], 10: [("H", 7, 0), ("H", 7, 1)], 12: [("H", 10, 0)]}
+MEMBER_ROUNDS = (0, 2, 4, 5)
+SCALAR_LAG = 4
+VECTOR_LAG = 2
 
 
 def tile_smoothed_target_encoding_k2_kernel(
@@ -38,30 +40,27 @@ def tile_smoothed_target_encoding_k2_kernel(
 
     with ExitStack() as ctx:
         keep = ctx.enter_context(tc.tile_pool(name="keep", bufs=1))
-        ring = ctx.enter_context(tc.tile_pool(name="ring", bufs=3))
+        ring = ctx.enter_context(tc.tile_pool(name="ring", bufs=2))
         psum = ctx.enter_context(tc.psum_pool(name="psum", bufs=8))
         ctx.enter_context(tc.manual_schedule())
 
         def bank():
             return psum.tile([P, W], F32, name="bank")
 
-        def rows_of_group(tensor, g, col0, width):
-            return tensor[g * W : (g + 1) * W, col0 : col0 + width].rearrange("(p t) c -> p t c", t=PACK)
+        def by_slot(tensor, group, col0, width):
+            rows = tensor[group * W : (group + 1) * W, col0 : col0 + width]
+            return rows.rearrange("(p t) c -> p t c", t=PACK)
 
         smooth_rows = keep.tile([P, P], BF16, name="smooth_rows")
         nc.vector.memset(smooth_rows[:], 0.0)
         d_scales = keep.tile([P, PASSES, T], U8, name="d_scales", align_bytes=64)
         nc.vector.memset(d_scales[:].bitcast(I32), 0)
-        warm = keep.tile([P, 1], F32, name="warm")
-        nc.vector.memset(warm[:], 1.0)
 
         count_bf = keep.tile([P, GROUPS, PACK], BF16, name="count_bf")
         nc.scalar.dma_start(out=count_bf[:], in_=counts.rearrange("(g p t) -> p g t", g=GROUPS, t=PACK))
-        smooth_strips = smooth.rearrange("(b j) -> b j", j=P)
+        smooth_strips = smooth.rearrange("(s j) -> s j", j=P)
         nc.scalar.dma_start(out=smooth_rows[0:8, :], in_=smooth_strips[0:8, :])
         nc.scalar.dma_start(out=smooth_rows[8:STRIPS, :], in_=smooth_strips[8:STRIPS, :])
-        warm_out = keep.tile([P, 1], F32, name="warm_out")
-        nc.scalar.activation(out=warm_out[:], in_=warm[:], func=ACT.Ln)
 
         ident_bf = keep.tile([P, P], BF16, name="ident_bf")
         make_identity(nc, ident_bf[:])
@@ -69,60 +68,58 @@ def tile_smoothed_target_encoding_k2_kernel(
         make_identity(nc, ident_f32[:])
 
         member_raw = {}
-        d_head = {}
         prior_sb = {}
+        d_codes = {}
+        d_words = target_words.rearrange("k p n t -> p k (n t)").bitcast(I32)
 
         def load_member(g, k):
-            member_raw[g, k] = keep.tile([P, PACK, W], BF16, name="member_raw_%d_%d" % (g, k))
-            nc.sync.dma_start(out=member_raw[g, k][:], in_=rows_of_group(member, k, g * W, W))
+            place = "member_raw_%d_%d" % (g, k)
+            member_raw[g, k] = keep.tile([P, PACK, W], BF16, name=place, tag=place)
+            nc.sync.dma_start(out=member_raw[g, k][:], in_=by_slot(member, k, g * W, W))
 
-        def load_prior(g, b):
-            prior_sb[g, b] = keep.tile([P, PACK, W], BF16, name="prior_%d_%d" % (g, b))
-            nc.sync.dma_start(out=prior_sb[g, b][:], in_=rows_of_group(prior, g, b * W, W))
-
-        d_words = target_words.rearrange("k p n t -> p k (n t)").bitcast(I32)
-        head_w = HEAD_BLOCKS * W
-        def load_d_head(k):
-            d_head[k] = keep.tile([P, head_w], U32, name="d_head_%d" % k, align_bytes=64)
-            nc.sync.dma_start(out=d_head[k][:].bitcast(I32), in_=d_words[:, k, 0:head_w])
+        def load_prior(g, b, place):
+            prior_sb[g, b] = keep.tile([P, PACK, W], BF16, name="prior_%d_%d" % (g, b), tag=place)
+            nc.sync.dma_start(out=prior_sb[g, b][:], in_=by_slot(prior, g, b * W, W))
 
         def load_d_scales(col0, width):
-            for q in range(4):
+            for q in range(QUADRANTS):
+                rows = target_scales[:, 4 * q : 4 * q + 4, col0 : col0 + width].rearrange("k r n -> r k n")
                 nc.sync.dma_start(
-                    out=d_scales[32 * q : 32 * q + 4, :, col0 : col0 + width].bitcast(I32),
-                    in_=target_scales[:, 4 * q : 4 * q + 4, col0 : col0 + width].rearrange("k r n -> r k n").bitcast(I32),
+                    out=d_scales[32 * q : 32 * q + 4, :, col0 : col0 + width].bitcast(I32), in_=rows.bitcast(I32)
                 )
 
-        load_member(0, 0)
-        load_d_scales(0, head_w)
-        load_d_head(0)
-        for k in range(1, PASSES):
-            load_member(0, k)
-            load_d_head(k)
-        d_rest = {}
+        def load_d_pass(k, b):
+            words = keep.tile([P, W], U32, name="d_codes_%d_%d" % (k, b), align_bytes=64)
+            nc.sync.dma_start(out=words[:].bitcast(I32), in_=d_words[:, k, b * W : (b + 1) * W])
+            d_codes[k, b] = words[:]
 
         def load_d_block(b):
-            d_rest[b] = keep.tile([P, PASSES, W], U32, name="d_block_%d" % b, align_bytes=64)
-            nc.sync.dma_start(out=d_rest[b][:].bitcast(I32), in_=d_words[:, :, b * W : (b + 1) * W])
+            words = keep.tile([P, PASSES, W], U32, name="d_block_%d" % b, align_bytes=64)
+            nc.sync.dma_start(out=words[:].bitcast(I32), in_=d_words[:, :, b * W : (b + 1) * W])
+            for k in range(PASSES):
+                d_codes[k, b] = words[:, k, :]
 
-        load_prior(0, 0)
+        load_member(0, 0)
+        load_d_scales(0, HEAD_BLOCKS * W)
+        load_d_pass(0, 0)
+        load_member(0, 1)
+        load_d_pass(0, 1)
+        load_member(0, 2)
+        load_d_pass(1, 0)
+        load_d_pass(1, 1)
+        load_member(0, 3)
+        for k in range(2, PASSES):
+            load_d_pass(k, 0)
+            load_d_pass(k, 1)
         load_member(1, 0)
-        load_prior(0, 1)
+        load_prior(0, 0, "prior_first")
+        load_prior(0, 1, "prior_second")
         load_member(1, 1)
-        load_d_scales(head_w, T - head_w)
-        load_d_block(2)
+        load_d_scales(HEAD_BLOCKS * W, W)
+        load_d_block(HEAD_BLOCKS)
         load_member(1, 2)
         load_member(1, 3)
-        load_prior(0, 2)
-        for b in range(BLOCKS):
-            load_prior(1, b)
 
-        def d_codes(k, col0, width):
-            if col0 < head_w:
-                return d_head[k][:, col0 : col0 + width].bitcast(E5M2X4)
-            return d_rest[col0 // W][:, k, col0 % W : col0 % W + width].bitcast(E5M2X4)
-
-        ln_smooth = keep.tile([P, T], F32, name="ln_smooth")
         spread = [bank() for b in range(BLOCKS)]
         for s in range(STRIPS):
             nc.tensor.matmul(
@@ -132,70 +129,80 @@ def tile_smoothed_target_encoding_k2_kernel(
                 start=True,
                 stop=True,
             )
-        turned = bank()
-        nc.tensor.matmul(out=turned[:, 0:16], lhsT=smooth_rows[:], rhs=ident_bf[:, 0:16], start=True, stop=True)
-        inv_smooth = keep.tile([P, STRIPS], F32, name="inv_smooth")
+        smooth_cols = bank()
+        nc.tensor.matmul(
+            out=smooth_cols[:, 0:STRIPS], lhsT=smooth_rows[:], rhs=ident_bf[:, 0:STRIPS], start=True, stop=True
+        )
         count_cols = count_bf[:].rearrange("p g t -> p (g t)")
-        inv_count = keep.tile([P, GROUPS * PACK], F32, name="inv_count")
         ln_count = keep.tile([P, GROUPS * PACK], F32, name="ln_count")
         nc.scalar.activation(out=ln_count[:], in_=count_cols, func=ACT.Ln)
+        ln_smooth = keep.tile([P, T], F32, name="ln_smooth")
         for b in range(BLOCKS):
             nc.scalar.activation(out=ln_smooth[:, b * W : (b + 1) * W], in_=spread[b][:], func=ACT.Ln)
         neg_ln_count = keep.tile([P, GROUPS * PACK], F32, name="neg_ln_count")
+        inv_count = keep.tile([P, GROUPS * PACK], F32, name="inv_count")
+        inv_smooth = keep.tile([P, STRIPS], F32, name="inv_smooth")
 
+        def small_vector_work():
+            nc.vector.tensor_scalar(out=neg_ln_count[:], in0=ln_count[:], scalar1=-1.0, scalar2=None, op0=ALU.mult)
+            nc.vector.reciprocal(out=inv_smooth[:], in_=smooth_cols[:, 0:STRIPS])
+            nc.vector.reciprocal(out=inv_count[:], in_=count_cols)
+
+        grouped = {}
         member_codes = {}
         member_scales = {}
-        grouped = {}
-
-        def interleave(g, k, h, engine):
-            if g == 0:
-                grouped[g, k, h] = ring.tile([P, HALF, PACK], BF16, name="grouped_half", bufs=2, align_bytes=64)
-                src = member_raw[g, k][:, :, h * HALF : (h + 1) * HALF].rearrange("p j (c i) -> p c j i", i=4)
-                dst = grouped[g, k, h][:].rearrange("p (c i) j -> p c j i", i=4)
-            else:
-                grouped[g, k, h] = ring.tile([P, W, PACK], BF16, name="grouped", bufs=2, align_bytes=64)
-                src = member_raw[g, k][:].rearrange("p j (m e t) -> p m t e j", e=2, t=PACK)
-                dst = grouped[g, k, h][:].rearrange("p (t m e) j -> p m t e j", t=PACK, e=2)
-            nc.vector.tensor_copy(out=dst, in_=src)
-
-        def quantise_member(g, k, h):
-            if (g, k) not in member_codes:
+        for g in range(GROUPS):
+            for k in range(PASSES):
                 member_codes[g, k] = keep.tile([P, W], U32, name="member_codes_%d_%d" % (g, k), align_bytes=64)
                 member_scales[g, k] = keep.tile([P, W], U8, name="member_scales_%d_%d" % (g, k), align_bytes=64)
-            cols = slice(0, W) if h is None else slice(h * HALF, (h + 1) * HALF)
+
+        def interleave_in_order(k, h):
+            grouped[0, k, h] = ring.tile([P, HALF, PACK], BF16, name="grouped_half", align_bytes=64)
+            raw = member_raw[0, k][:, :, h * HALF : (h + 1) * HALF]
+            nc.vector.tensor_copy(
+                out=grouped[0, k, h][:].rearrange("p (c i) j -> p c j i", i=4),
+                in_=raw.rearrange("p j (c i) -> p c j i", i=4),
+            )
+
+        def interleave_by_slot(k, copy, part):
+            if (1, k) not in grouped:
+                grouped[1, k] = ring.tile([P, W, PACK], BF16, name="grouped", align_bytes=64)
+            copy(
+                out=grouped[1, k][:].rearrange("p (t m e) j -> p m t e j", t=PACK, e=2)[:, part],
+                in_=member_raw[1, k][:].rearrange("p j (m e t) -> p m t e j", e=2, t=PACK)[:, part],
+            )
+
+        def quantise_member(g, k, cols, source):
             nc.vector.quantize_mx(
                 out=member_codes[g, k][:, cols].bitcast(E4M3X4),
                 scales=member_scales[g, k][:, cols],
-                in_=grouped[g, k, h][:].rearrange("p c j -> p (c j)"),
+                in_=source[:].rearrange("p c j -> p (c j)"),
             )
 
-        turned_blocks = [(0, 0), (0, 1), (0, 2), (1, 1), (1, 2)]
         weight = {}
 
-        def make_weight(g, b, t, blocks):
-            if t == 0:
-                tile = ring.tile([P, PACK, blocks * W], F32, name="weight_%d" % blocks, bufs=2 // blocks)
-                for extra in range(blocks):
-                    weight[g, b + extra] = tile[:, :, extra * W : (extra + 1) * W]
-                weight[g, b, blocks] = tile
+        def weight_tile(g, b, blocks):
+            tile = ring.tile([P, PACK, blocks * W], F32, name="weight_%d" % blocks)
+            for n in range(blocks):
+                weight[g, b + n] = tile[:, :, n * W : (n + 1) * W]
+            return tile
+
+        def make_weight(tile, g, b, t):
             col = g * PACK + t
-            if (g, b) in turned_blocks:
-                bias, scale = neg_ln_count[:, col : col + 1], 1.0
-            else:
-                bias, scale = ln_count[:, col : col + 1], -1.0
+            direct = (g, b) == DIRECT_BLOCK
             nc.scalar.activation(
-                out=weight[g, b, blocks][:, t, :],
-                in_=ln_smooth[:, b * W : (b + blocks) * W],
+                out=tile[:, t, :],
+                in_=ln_smooth[:, b * W : b * W + tile.shape[2]],
                 func=ACT.Sigmoid,
-                bias=bias,
-                scale=scale,
+                bias=(ln_count if direct else neg_ln_count)[:, col : col + 1],
+                scale=-1.0 if direct else 1.0,
             )
 
         sums = {}
         scaled = {}
         joined = {}
-        y_tile = {}
         shrunk_prior = {}
+        y_tile = {}
         y_bf = {}
         y_codes = [keep.tile([P, T], U32, name="y_codes_%d" % g, align_bytes=64) for g in range(GROUPS)]
         y_scales = [keep.tile([P, T], U8, name="y_scales_%d" % g, align_bytes=64) for g in range(GROUPS)]
@@ -204,75 +211,88 @@ def tile_smoothed_target_encoding_k2_kernel(
             g, b, i = unit
             if k == 0:
                 sums[unit] = bank()
-            if (g, b) in turned_blocks:
-                col0 = b * W + i * P
-                nc.tensor.matmul_mx(
-                    out=sums[unit][:],
-                    lhsT=d_codes(k, col0, P),
-                    lhsT_scale=d_scales[:, k, col0 : col0 + P],
-                    rhs=member_codes[g, k][:].bitcast(E4M3X4),
-                    rhs_scale=member_scales[g, k][:],
-                    start=(k == 0),
-                    stop=(k == PASSES - 1),
-                )
+            strip = slice(i * P, (i + 1) * P)
+            m_words, m_scales = member_codes[g, k], member_scales[g, k]
+            d_block_scales = d_scales[:, k, b * W : (b + 1) * W]
+            if (g, b) == DIRECT_BLOCK:
+                lhs, lhs_scale = m_words[:, strip].bitcast(E4M3X4), m_scales[:, strip]
+                rhs, rhs_scale = d_codes[k, b].bitcast(E5M2X4), d_block_scales
             else:
-                nc.tensor.matmul_mx(
-                    out=sums[unit][:],
-                    lhsT=member_codes[g, k][:, i * P : (i + 1) * P].bitcast(E4M3X4),
-                    lhsT_scale=member_scales[g, k][:, i * P : (i + 1) * P],
-                    rhs=d_codes(k, b * W, W),
-                    rhs_scale=d_scales[:, k, b * W : (b + 1) * W],
-                    start=(k == 0),
-                    stop=(k == PASSES - 1),
-                )
+                lhs, lhs_scale = d_codes[k, b][:, strip].bitcast(E5M2X4), d_block_scales[:, strip]
+                rhs, rhs_scale = m_words[:].bitcast(E4M3X4), m_scales[:]
+            nc.tensor.matmul_mx(
+                out=sums[unit][:],
+                lhsT=lhs,
+                lhsT_scale=lhs_scale,
+                rhs=rhs,
+                rhs_scale=rhs_scale,
+                start=(k == 0),
+                stop=(k == PASSES - 1),
+            )
 
         def scale_out(unit):
             g, b, i = unit
             scaled[unit] = ring.tile([P, PACK, P], F32, name="scaled", bufs=4)
-            if g == 0:
-                src = sums[unit][:].rearrange("p (m t) -> p t m", t=PACK)
-            else:
-                src = sums[unit][:].rearrange("p (t m) -> p t m", t=PACK)
+            order = "p (m t) -> p t m" if g == 0 else "p (t m) -> p t m"
             strip = b * PACK + i
-            nc.scalar.activation(out=scaled[unit][:], in_=src, func=ACT.Copy, scale=inv_smooth[:, strip : strip + 1])
-
-        def lay_prior(unit):
-            g, b, i = unit
-            joined[unit] = bank()
-            nc.tensor.matmul(
-                out=joined[unit][:].rearrange("p (t j) -> p t j", t=PACK),
-                lhsT=ident_bf[:],
-                rhs=prior_sb[g, b][:, :, i * P : (i + 1) * P],
-                start=True,
-                stop=False,
+            nc.scalar.activation(
+                out=scaled[unit][:],
+                in_=sums[unit][:].rearrange(order, t=PACK),
+                func=ACT.Copy,
+                scale=inv_smooth[:, strip : strip + 1],
             )
 
-        def turn_and_add(unit):
-            for t in range(PACK):
+        def turn_and_add(units):
+            for unit in units:
+                g, b, i = unit
+                joined[unit] = bank()
                 nc.tensor.matmul(
-                    out=joined[unit][:, t * P : (t + 1) * P],
-                    lhsT=scaled[unit][:, t, :],
-                    rhs=ident_f32[:],
-                    is_transpose=True,
-                    start=False,
-                    stop=(t == PACK - 1),
+                    out=joined[unit][:].rearrange("p (t j) -> p t j", t=PACK),
+                    lhsT=ident_bf[:],
+                    rhs=prior_sb[g, b][:, :, i * P : (i + 1) * P],
+                    start=True,
+                    stop=False,
                 )
+            for unit in units:
+                for t in range(PACK):
+                    nc.tensor.matmul(
+                        out=joined[unit][:, t * P : (t + 1) * P],
+                        lhsT=scaled[unit][:, t, :],
+                        rhs=ident_f32[:],
+                        is_transpose=True,
+                        start=False,
+                        stop=(t == PACK - 1),
+                    )
 
-        def weigh(unit):
+        def weigh_joined(unit):
             g, b, i = unit
             if i % 2 == 0:
-                y_tile[g, b, i // 2] = ring.tile([P, PACK, HALF], F32, name="y_half", bufs=6)
-            c0 = (i % 2) * P
+                y_tile[g, b, i // 2] = ring.tile([P, PACK, HALF], F32, name="y_half", bufs=6)[:]
             nc.vector.tensor_tensor(
-                out=y_tile[g, b, i // 2][:, :, c0 : c0 + P],
+                out=y_tile[g, b, i // 2][:, :, (i % 2) * P : (i % 2 + 1) * P],
                 in0=joined[unit][:].rearrange("p (t j) -> p t j", t=PACK),
                 in1=weight[g, b][:, :, i * P : (i + 1) * P],
                 op=ALU.mult,
             )
 
+        y_direct = keep.tile([P, PACK, W], F32, name="y_direct")
+        for h in range(2):
+            y_tile[DIRECT_BLOCK + (h,)] = y_direct[:, :, h * HALF : (h + 1) * HALF]
+
+        def weigh_sums(unit):
+            g, b, t = unit
+            nc.vector.scalar_tensor_tensor(
+                out=y_direct[:, t, :],
+                in0=sums[unit][:],
+                scalar=inv_count[:, g * PACK + t : g * PACK + t + 1],
+                in1=weight[g, b][:, t, :],
+                op0=ALU.mult,
+                op1=ALU.mult,
+            )
+
         def shrink_prior(unit):
             g, b, t = unit
-            shrunk_prior[unit] = ring.tile([P, W], F32, name="shrunk_prior", bufs=2)
+            shrunk_prior[unit] = ring.tile([P, W], F32, name="shrunk_prior")
             nc.vector.scalar_tensor_tensor(
                 out=shrunk_prior[unit][:],
                 in0=weight[g, b][:, t, :],
@@ -282,179 +302,183 @@ def tile_smoothed_target_encoding_k2_kernel(
                 op1=ALU.mult,
             )
 
-        def weigh_sums(unit):
-            g, b, t = unit
-            if t == 0:
-                y_tile[g, b] = ring.tile([P, PACK, W], F32, name="y_block", bufs=1)
-            col = g * PACK + t
-            nc.vector.scalar_tensor_tensor(
-                out=y_tile[g, b][:, t, :],
-                in0=sums[unit][:],
-                scalar=inv_count[:, col : col + 1],
-                in1=weight[g, b][:, t, :],
-                op0=ALU.mult,
-                op1=ALU.mult,
-            )
-
         def join_prior(unit):
-            g, b, t = unit
-            row = y_tile[g, b][:, t, :]
+            row = y_direct[:, unit[2], :]
             nc.vector.tensor_tensor(out=row, in0=row, in1=shrunk_prior[unit][:], op=ALU.subtract)
 
-        def round_y(g, col0, width, source, engine):
-            tile = ring.tile([P, HALF, PACK], BF16, name="y_bf", bufs=5, align_bytes=64)
-            y_bf[g, col0] = tile
-            src = source.rearrange("p t (c i) -> p c t i", i=4)
-            dst = tile[:, 0:width, :].rearrange("p (c i) t -> p c t i", i=4)
-            if engine == "vector":
-                nc.vector.tensor_copy(out=dst, in_=src)
-            else:
-                nc.scalar.copy(out=dst, in_=src)
+        def round_y(copy, g, col0, source):
+            width = source.shape[2]
+            y_bf[g, col0] = ring.tile([P, HALF, PACK], BF16, name="y_bf", bufs=5, align_bytes=64)[:, 0:width, :]
+            copy(
+                out=y_bf[g, col0].rearrange("p (c i) t -> p c t i", i=4),
+                in_=source.rearrange("p t (c i) -> p c t i", i=4),
+            )
 
-        def quantise_y(g, col0, width):
+        def quantise_y(g, col0):
+            width = y_bf[g, col0].shape[1]
             nc.vector.quantize_mx(
                 out=y_codes[g][:, col0 : col0 + width].bitcast(E4M3X4),
                 scales=y_scales[g][:, col0 : col0 + width],
-                in_=y_bf[g, col0][:, 0:width, :].rearrange("p c t -> p (c t)"),
+                in_=y_bf[g, col0].rearrange("p c t -> p (c t)"),
             )
+
+        def store_y(g, col0, source):
+            nc.sync.dma_start(out=by_slot(out_0, g, col0, source.shape[2]), in_=source)
 
         def store_codes(g, col0, width):
             words = out_1[g].rearrange("p m t -> p (m t)").bitcast(I32)
             nc.sync.dma_start(out=words[:, col0 : col0 + width], in_=y_codes[g][:, col0 : col0 + width].bitcast(I32))
 
         def store_scales(g, col0, width, queues):
-            for q in range(4):
+            for q in range(QUADRANTS):
                 queues[q % len(queues)].dma_start(
                     out=out_2[g, 4 * q : 4 * q + 4, col0 : col0 + width].bitcast(I32),
                     in_=y_scales[g][32 * q : 32 * q + 4, col0 : col0 + width].bitcast(I32),
                 )
 
-        def pair(g, b, h):
+        def first_col(half):
+            return half[1] * W + half[2] * HALF
+
+        def round_half(copy, half):
+            round_y(copy, half[0], first_col(half), y_tile[half])
+
+        def finish_half(half):
+            g, b, h = half
+            quantise_y(g, first_col(half))
+            if h == 1:
+                store_codes(g, b * W, W)
+            if half == (0, BLOCKS - 1, 1):
+                store_scales(0, 0, T, [nc.sync])
+
+        rounds = [(g, b, h) for g in range(GROUPS) for b in range(BLOCKS) for h in range(2)]
+        last = len(rounds) - 1
+        head_rounds = 2 * HEAD_BLOCKS
+        direct_rounds = [r for r in range(len(rounds)) if rounds[r][:2] == DIRECT_BLOCK]
+
+        def units_of(r):
+            g, b, h = rounds[r]
             return [(g, b, 2 * h), (g, b, 2 * h + 1)]
-
-        rounds = [pair(g, b, h) for g in range(GROUPS) for b in range(BLOCKS) for h in range(2)]
-
-        def is_turned(r):
-            return 0 <= r < len(rounds) and rounds[r][0][:2] in turned_blocks
-
-        def is_plain(r):
-            return 0 <= r < len(rounds) and not is_turned(r)
 
         for k in range(PASSES):
             for h in range(2):
-                interleave(0, k, h, "vector")
+                interleave_in_order(k, h)
             for h in range(2):
-                quantise_member(0, k, h)
+                quantise_member(0, k, slice(h * HALF, (h + 1) * HALF), grouped[0, k, h])
             if k == 0:
-                nc.vector.tensor_scalar(out=neg_ln_count[:], in0=ln_count[:], scalar1=-1.0, scalar2=None, op0=ALU.mult)
-                nc.vector.reciprocal(out=inv_smooth[:], in_=turned[:, 0:STRIPS])
-                nc.vector.reciprocal(out=inv_count[:], in_=count_cols)
-                for t in range(PACK):
-                    make_weight(0, 0, t, 2)
-                for t in range(PACK):
-                    make_weight(0, 2, t, 1)
+                small_vector_work()
             if k < PASSES - 1:
-                for r in range(HEAD_ROUNDS):
-                    for unit in rounds[r]:
+                for r in range(head_rounds):
+                    for unit in units_of(r):
                         mx_pass(unit, k)
 
-        last = len(rounds) - 1
+        for b, blocks in ((0, HEAD_BLOCKS), (HEAD_BLOCKS, 1)):
+            tile = weight_tile(0, b, blocks)
+            for t in range(PACK):
+                make_weight(tile, 0, b, t)
+        direct_weight = weight_tile(1, 0, 1)
+        late_weight = weight_tile(1, 1, 2)
 
-        def half(r, h=0):
-            g, b, i = rounds[r][0]
-            if is_turned(r):
-                return g, b * W + i * P, y_tile[g, b, i // 2][:]
-            return g, b * W + h * HALF, y_tile[g, b][:, :, h * HALF : (h + 1) * HALF]
+        for k, (g, b) in enumerate([(0, 2), (1, 0), (1, 1), (1, 2)]):
+            load_prior(g, b, "member_raw_0_%d" % k)
 
-        def finish(r, h=0):
-            g, col0, y = half(r, h)
-            quantise_y(g, col0, HALF)
-            if col0 % W:
-                store_codes(g, col0 - HALF, W)
-            if (g, col0) == (0, T - HALF):
-                store_scales(g, 0, T, [nc.sync])
+        all_pairs, low_pairs, high_pairs = slice(0, P // 2), slice(0, P // 4), slice(P // 4, P // 2)
+        rounded_on_scalar = []
 
-        jobs = JOBS
-        rounded = []
+        def scalar_round_half(half):
+            round_half(nc.scalar.copy, half)
+            rounded_on_scalar.append(half)
 
-        def spare_job(job):
-            if job[0] == "w":
-                make_weight(job[1], job[2], job[3], 1)
-                make_weight(job[1], job[2], job[3] + 1, 1)
-            elif job[0] == "W":
-                make_weight(1, 1, job[1], 2)
-            else:
-                g, col0, y = half(job[1], job[2])
-                round_y(g, col0, HALF, y, "scalar")
-                rounded.append(job[1:])
+        def scalar_jobs(r):
+            jobs = []
+            if r == MEMBER_ROUNDS[-1]:
+                jobs.append(lambda: interleave_by_slot(PASSES - 1, nc.scalar.copy, high_pairs))
+            if r + 3 in direct_rounds:
+                slots = [unit[2] for unit in units_of(r + 3)]
+                jobs.append(lambda: [make_weight(direct_weight, 1, 0, t) for t in slots])
+            if r in direct_rounds:
+                for unit in units_of(r):
+                    jobs.append(lambda t=unit[2]: make_weight(late_weight, 1, 1, t))
+            if 0 <= r - SCALAR_LAG < direct_rounds[0]:
+                jobs.append(lambda: scalar_round_half(rounds[r - SCALAR_LAG]))
+            if r - VECTOR_LAG - 1 == direct_rounds[-1]:
+                jobs.append(lambda: scalar_round_half(DIRECT_BLOCK + (1,)))
+            return jobs
 
-        for r in range(len(rounds) + 1):
-            if r <= last:
-                for unit in rounds[r]:
-                    for k in range(PASSES - 1 if r < HEAD_ROUNDS else 0, PASSES):
-                        mx_pass(unit, k)
-            member_pass = MP.get(r)
-            on_vector = r - 2 in HV
-            to_finish = list(rounded)
-            rounded.clear()
-            todo = jobs.get(r, [])
-            for job in todo[:1]:
-                spare_job(job)
-            if is_turned(r):
-                scale_out(rounds[r][0])
-            for job in todo[1:2]:
-                spare_job(job)
-            if is_turned(r):
-                scale_out(rounds[r][1])
-            for job in todo[2:]:
-                spare_job(job)
-            if is_turned(r - 1):
-                for unit in rounds[r - 1]:
-                    lay_prior(unit)
-                for unit in rounds[r - 1]:
-                    turn_and_add(unit)
-            if on_vector:
-                g, col0, y = half(r - 2)
-                round_y(g, col0, HALF, y, "vector")
-            if member_pass is not None:
-                interleave(1, member_pass, None, "vector")
-            if r > last:
-                break
-            for done in to_finish:
-                finish(*done)
-            if member_pass is not None:
-                quantise_member(1, member_pass, None)
-            if on_vector:
-                finish(r - 2)
-            if is_plain(r):
-                weigh_sums(rounds[r][0])
-                weigh_sums(rounds[r][1])
-            if is_turned(r - 1):
-                weigh(rounds[r - 1][0])
-                weigh(rounds[r - 1][1])
-                g, col0, y = half(r - 1)
-                nc.sync.dma_start(out=rows_of_group(out_0, g, col0, HALF), in_=y)
-            if is_plain(r):
-                shrink_prior(rounds[r][0])
-                shrink_prior(rounds[r][1])
-                join_prior(rounds[r][0])
-                join_prior(rounds[r][1])
-                g, b, i = rounds[r][0]
+        def vector_half(r):
+            done = r - VECTOR_LAG
+            if done == direct_rounds[-1]:
+                return [DIRECT_BLOCK + (0,)]
+            return [rounds[done]] if done > direct_rounds[-1] else []
+
+        for r in range(len(rounds)):
+            units = units_of(r)
+            direct = r in direct_rounds
+            before = units_of(r - 1) if r > 0 and r - 1 not in direct_rounds else []
+            passes = range(PASSES - 1 if r < head_rounds else 0, PASSES)
+            early, late = (units[:1], units[1:]) if r == last else (units, [])
+            for unit in early:
+                for k in passes:
+                    mx_pass(unit, k)
+
+            to_finish = list(rounded_on_scalar)
+            rounded_on_scalar.clear()
+            jobs = scalar_jobs(r)
+            for n in range(max(len(jobs), len(early))):
+                for job in jobs[n : n + 1]:
+                    job()
+                if not direct and n < len(early):
+                    scale_out(early[n])
+
+            turn_and_add(before)
+            for unit in late:
+                for k in passes:
+                    mx_pass(unit, k)
+                scale_out(unit)
+
+            for half in vector_half(r):
+                round_half(nc.vector.tensor_copy, half)
+            if r in MEMBER_ROUNDS:
+                k = MEMBER_ROUNDS.index(r)
+                interleave_by_slot(k, nc.vector.tensor_copy, low_pairs if k == PASSES - 1 else all_pairs)
+            for half in to_finish:
+                finish_half(half)
+            if r in MEMBER_ROUNDS:
+                quantise_member(1, k, slice(0, W), grouped[1, k])
+            for half in vector_half(r):
+                finish_half(half)
+            if direct:
+                for unit in units:
+                    weigh_sums(unit)
+            for unit in before:
+                weigh_joined(unit)
+            if before:
+                store_y(rounds[r - 1][0], first_col(rounds[r - 1]), y_tile[rounds[r - 1]])
+            if direct:
+                for unit in units:
+                    shrink_prior(unit)
+                for unit in units:
+                    join_prior(unit)
+                slots = slice(units[0][2], units[1][2] + 1)
                 nc.sync.dma_start(
-                    out=rows_of_group(out_0, g, b * W, W)[:, i : i + 2, :], in_=y_tile[g, b][:, i : i + 2, :]
+                    out=by_slot(out_0, DIRECT_BLOCK[0], DIRECT_BLOCK[1] * W, W)[:, slots, :], in_=y_direct[:, slots, :]
                 )
-        for done in to_finish:
-            finish(*done)
-        store_scales(1, 0, T - W, [nc.sync])
-        weigh(rounds[last][0])
-        g, col0, y = half(last)
-        nc.sync.dma_start(out=rows_of_group(out_0, g, col0, P), in_=y[:, :, 0:P])
-        weigh(rounds[last][1])
-        nc.sync.dma_start(out=rows_of_group(out_0, g, col0 + P, P), in_=y[:, :, P:HALF])
-        round_y(g, col0, P, y[:, :, 0:P], "scalar")
-        round_y(g, col0 + P, P, y[:, :, P:HALF], "vector")
-        quantise_y(g, col0 - HALF, HALF)
-        quantise_y(g, col0, P)
-        quantise_y(g, col0 + P, P)
-        store_codes(g, col0 - HALF, W)
+
+        g = GROUPS - 1
+        turn_and_add(units_of(last))
+        round_half(nc.vector.tensor_copy, rounds[last - 1])
+        store_scales(g, 0, T - W, [nc.sync])
+        first, second = units_of(last)
+        col0 = first_col(rounds[last])
+        weigh_joined(first)
+        quantise_y(g, col0 - HALF)
+        store_codes(g, col0 - HALF, HALF)
+        y_last = y_tile[rounds[last]]
+        store_y(g, col0, y_last[:, :, 0:P])
+        weigh_joined(second)
+        store_y(g, col0 + P, y_last[:, :, P:HALF])
+        round_y(nc.scalar.copy, g, col0, y_last[:, :, 0:P])
+        round_y(nc.vector.tensor_copy, g, col0 + P, y_last[:, :, P:HALF])
+        quantise_y(g, col0)
+        quantise_y(g, col0 + P)
+        store_codes(g, col0, HALF)
         store_scales(g, T - W, W, [nc.scalar, nc.sync])

@@ -29,7 +29,7 @@ QUADRANTS = 4
 DIRECT_BLOCK = (1, 0)
 HEAD_BLOCKS = 2
 MEMBER_ROUNDS = (0, 2, 4, 5)
-SCALAR_LAG = 4
+SCALAR_LAG = 3
 VECTOR_LAG = 2
 
 
@@ -73,13 +73,14 @@ def tile_smoothed_target_encoding_k2_kernel(
         d_words = target_words.rearrange("k p n t -> p k (n t)").bitcast(I32)
 
         def load_member(g, k):
-            place = "member_raw_%d_%d" % (g, k)
-            member_raw[g, k] = keep.tile([P, PACK, W], BF16, name=place, tag=place)
+            member_raw[g, k] = keep.tile([P, PACK, W], BF16, name="member_raw_%d_%d" % (g, k))
             nc.sync.dma_start(out=member_raw[g, k][:], in_=by_slot(member, k, g * W, W))
 
-        def load_prior(g, b, place):
-            prior_sb[g, b] = keep.tile([P, PACK, W], BF16, name="prior_%d_%d" % (g, b), tag=place)
-            nc.sync.dma_start(out=prior_sb[g, b][:], in_=by_slot(prior, g, b * W, W))
+        def load_prior(g, b0, blocks):
+            tile = keep.tile([P, PACK, blocks * W], BF16, name="prior_%d_%d" % (g, b0))
+            nc.sync.dma_start(out=tile[:], in_=by_slot(prior, g, b0 * W, blocks * W))
+            for n in range(blocks):
+                prior_sb[g, b0 + n] = tile[:, :, n * W : (n + 1) * W]
 
         def load_d_scales(col0, width):
             for q in range(QUADRANTS):
@@ -88,10 +89,11 @@ def tile_smoothed_target_encoding_k2_kernel(
                     out=d_scales[32 * q : 32 * q + 4, :, col0 : col0 + width].bitcast(I32), in_=rows.bitcast(I32)
                 )
 
-        def load_d_pass(k, b):
-            words = keep.tile([P, W], U32, name="d_codes_%d_%d" % (k, b), align_bytes=64)
-            nc.sync.dma_start(out=words[:].bitcast(I32), in_=d_words[:, k, b * W : (b + 1) * W])
-            d_codes[k, b] = words[:]
+        def load_d_head(k):
+            words = keep.tile([P, HEAD_BLOCKS * W], U32, name="d_head_%d" % k, align_bytes=64)
+            nc.sync.dma_start(out=words[:].bitcast(I32), in_=d_words[:, k, 0 : HEAD_BLOCKS * W])
+            for b in range(HEAD_BLOCKS):
+                d_codes[k, b] = words[:, b * W : (b + 1) * W]
 
         def load_d_block(b):
             words = keep.tile([P, PASSES, W], U32, name="d_block_%d" % b, align_bytes=64)
@@ -99,26 +101,20 @@ def tile_smoothed_target_encoding_k2_kernel(
             for k in range(PASSES):
                 d_codes[k, b] = words[:, k, :]
 
-        load_member(0, 0)
-        load_d_scales(0, HEAD_BLOCKS * W)
-        load_d_pass(0, 0)
-        load_member(0, 1)
-        load_d_pass(0, 1)
-        load_member(0, 2)
-        load_d_pass(1, 0)
-        load_d_pass(1, 1)
-        load_member(0, 3)
-        for k in range(2, PASSES):
-            load_d_pass(k, 0)
-            load_d_pass(k, 1)
+        for k in range(PASSES):
+            load_member(0, k)
+            if k == 0:
+                load_d_scales(0, HEAD_BLOCKS * W)
+            load_d_head(k)
         load_member(1, 0)
-        load_prior(0, 0, "prior_first")
-        load_prior(0, 1, "prior_second")
+        load_prior(0, 0, HEAD_BLOCKS)
         load_member(1, 1)
         load_d_scales(HEAD_BLOCKS * W, W)
         load_d_block(HEAD_BLOCKS)
         load_member(1, 2)
         load_member(1, 3)
+        load_prior(0, HEAD_BLOCKS, 1)
+        load_prior(1, 0, BLOCKS)
 
         spread = [bank() for b in range(BLOCKS)]
         for s in range(STRIPS):
@@ -182,7 +178,7 @@ def tile_smoothed_target_encoding_k2_kernel(
         weight = {}
 
         def weight_tile(g, b, blocks):
-            tile = ring.tile([P, PACK, blocks * W], F32, name="weight_%d" % blocks)
+            tile = ring.tile([P, PACK, blocks * W], F32, name="weight_%d" % blocks, bufs=2 // blocks)
             for n in range(blocks):
                 weight[g, b + n] = tile[:, :, n * W : (n + 1) * W]
             return tile
@@ -202,6 +198,7 @@ def tile_smoothed_target_encoding_k2_kernel(
         scaled = {}
         joined = {}
         shrunk_prior = {}
+        y_block = {}
         y_tile = {}
         y_bf = {}
         y_codes = [keep.tile([P, T], U32, name="y_codes_%d" % g, align_bytes=64) for g in range(GROUPS)]
@@ -232,7 +229,7 @@ def tile_smoothed_target_encoding_k2_kernel(
 
         def scale_out(unit):
             g, b, i = unit
-            scaled[unit] = ring.tile([P, PACK, P], F32, name="scaled", bufs=4)
+            scaled[unit] = ring.tile([P, PACK, P], F32, name="scaled", bufs=6)
             order = "p (m t) -> p t m" if g == 0 else "p (t m) -> p t m"
             strip = b * PACK + i
             nc.scalar.activation(
@@ -266,8 +263,10 @@ def tile_smoothed_target_encoding_k2_kernel(
 
         def weigh_joined(unit):
             g, b, i = unit
-            if i % 2 == 0:
-                y_tile[g, b, i // 2] = ring.tile([P, PACK, HALF], F32, name="y_half", bufs=6)[:]
+            if i == 0:
+                y_block[g, b] = ring.tile([P, PACK, W], F32, name="y_turned", bufs=3)
+                for h in range(2):
+                    y_tile[g, b, h] = y_block[g, b][:, :, h * HALF : (h + 1) * HALF]
             nc.vector.tensor_tensor(
                 out=y_tile[g, b, i // 2][:, :, (i % 2) * P : (i % 2 + 1) * P],
                 in0=joined[unit][:].rearrange("p (t j) -> p t j", t=PACK),
@@ -349,6 +348,8 @@ def tile_smoothed_target_encoding_k2_kernel(
                 store_codes(g, b * W, W)
             if half == (0, BLOCKS - 1, 1):
                 store_scales(0, 0, T, [nc.sync])
+            if half == (1, BLOCKS - 2, 1):
+                store_scales(1, 0, T - W, [nc.sync])
 
         rounds = [(g, b, h) for g in range(GROUPS) for b in range(BLOCKS) for h in range(2)]
         last = len(rounds) - 1
@@ -366,20 +367,16 @@ def tile_smoothed_target_encoding_k2_kernel(
                 quantise_member(0, k, slice(h * HALF, (h + 1) * HALF), grouped[0, k, h])
             if k == 0:
                 small_vector_work()
-            if k < PASSES - 1:
-                for r in range(head_rounds):
-                    for unit in units_of(r):
-                        mx_pass(unit, k)
+            for r in range(head_rounds):
+                for unit in units_of(r):
+                    mx_pass(unit, k)
 
         for b, blocks in ((0, HEAD_BLOCKS), (HEAD_BLOCKS, 1)):
             tile = weight_tile(0, b, blocks)
             for t in range(PACK):
                 make_weight(tile, 0, b, t)
         direct_weight = weight_tile(1, 0, 1)
-        late_weight = weight_tile(1, 1, 2)
-
-        for k, (g, b) in enumerate([(0, 2), (1, 0), (1, 1), (1, 2)]):
-            load_prior(g, b, "member_raw_0_%d" % k)
+        late_weight = []
 
         all_pairs, low_pairs, high_pairs = slice(0, P // 2), slice(0, P // 4), slice(P // 4, P // 2)
         rounded_on_scalar = []
@@ -396,11 +393,13 @@ def tile_smoothed_target_encoding_k2_kernel(
                 slots = [unit[2] for unit in units_of(r + 3)]
                 jobs.append(lambda: [make_weight(direct_weight, 1, 0, t) for t in slots])
             if r in direct_rounds:
+                if not late_weight:
+                    late_weight.append(weight_tile(1, 1, 2))
                 for unit in units_of(r):
-                    jobs.append(lambda t=unit[2]: make_weight(late_weight, 1, 1, t))
+                    jobs.append(lambda t=unit[2]: make_weight(late_weight[0], 1, 1, t))
             if 0 <= r - SCALAR_LAG < direct_rounds[0]:
                 jobs.append(lambda: scalar_round_half(rounds[r - SCALAR_LAG]))
-            if r - VECTOR_LAG - 1 == direct_rounds[-1]:
+            if r - VECTOR_LAG == direct_rounds[-1]:
                 jobs.append(lambda: scalar_round_half(DIRECT_BLOCK + (1,)))
             return jobs
 
@@ -414,7 +413,7 @@ def tile_smoothed_target_encoding_k2_kernel(
             units = units_of(r)
             direct = r in direct_rounds
             before = units_of(r - 1) if r > 0 and r - 1 not in direct_rounds else []
-            passes = range(PASSES - 1 if r < head_rounds else 0, PASSES)
+            passes = range(PASSES if r < head_rounds else 0, PASSES)
             early, late = (units[:1], units[1:]) if r == last else (units, [])
             for unit in early:
                 for k in passes:
@@ -451,8 +450,11 @@ def tile_smoothed_target_encoding_k2_kernel(
                     weigh_sums(unit)
             for unit in before:
                 weigh_joined(unit)
-            if before:
+            if before and rounds[r - 1][0] == GROUPS - 1:
                 store_y(rounds[r - 1][0], first_col(rounds[r - 1]), y_tile[rounds[r - 1]])
+            elif before and rounds[r - 1][2] == 1:
+                g, b, h = rounds[r - 1]
+                store_y(g, b * W, y_block[g, b][:])
             if direct:
                 for unit in units:
                     shrink_prior(unit)
@@ -466,16 +468,14 @@ def tile_smoothed_target_encoding_k2_kernel(
         g = GROUPS - 1
         turn_and_add(units_of(last))
         round_half(nc.vector.tensor_copy, rounds[last - 1])
-        store_scales(g, 0, T - W, [nc.sync])
         first, second = units_of(last)
         col0 = first_col(rounds[last])
         weigh_joined(first)
         quantise_y(g, col0 - HALF)
         store_codes(g, col0 - HALF, HALF)
         y_last = y_tile[rounds[last]]
-        store_y(g, col0, y_last[:, :, 0:P])
         weigh_joined(second)
-        store_y(g, col0 + P, y_last[:, :, P:HALF])
+        store_y(g, col0, y_last)
         round_y(nc.scalar.copy, g, col0, y_last[:, :, 0:P])
         round_y(nc.vector.tensor_copy, g, col0 + P, y_last[:, :, P:HALF])
         quantise_y(g, col0)

@@ -28,7 +28,7 @@ QUADRANTS = 4
 
 DIRECT_BLOCK = (1, 0)
 HEAD_BLOCKS = 2
-MEMBER_ROUNDS = (0, 2, 4, 5)
+MEMBER_ROUNDS = (2, 4, 5)
 SCALAR_LAG = 3
 VECTOR_LAG = 2
 
@@ -73,8 +73,14 @@ def tile_smoothed_target_encoding_k2_kernel(
         d_words = target_words.rearrange("k p n t -> p k (n t)").bitcast(I32)
 
         def load_member(g, k):
-            member_raw[g, k] = keep.tile([P, PACK, W], BF16, name="member_raw_%d_%d" % (g, k))
-            nc.sync.dma_start(out=member_raw[g, k][:], in_=by_slot(member, k, g * W, W))
+            member_raw[g, k] = keep.tile([P, PACK, W], BF16, name="member_raw_%d_%d" % (g, k))[:]
+            nc.sync.dma_start(out=member_raw[g, k], in_=by_slot(member, k, g * W, W))
+
+        def load_member_both_groups(k):
+            rows = keep.tile([P, PACK, C], BF16, name="member_rows_%d" % k)
+            nc.sync.dma_start(out=rows[:], in_=by_slot(member, k, 0, C))
+            for g in range(GROUPS):
+                member_raw[g, k] = rows[:, :, g * W : (g + 1) * W]
 
         def load_prior(g, b0, blocks):
             tile = keep.tile([P, PACK, blocks * W], BF16, name="prior_%d_%d" % (g, b0))
@@ -102,17 +108,19 @@ def tile_smoothed_target_encoding_k2_kernel(
                 d_codes[k, b] = words[:, k, :]
 
         for k in range(PASSES):
-            load_member(0, k)
+            if k < PASSES - 1:
+                load_member(0, k)
+            else:
+                load_member_both_groups(k)
             if k == 0:
                 load_d_scales(0, HEAD_BLOCKS * W)
             load_d_head(k)
-        load_member(1, 0)
         load_prior(0, 0, HEAD_BLOCKS)
-        load_member(1, 1)
+        load_member(1, 0)
         load_d_scales(HEAD_BLOCKS * W, W)
         load_d_block(HEAD_BLOCKS)
+        load_member(1, 1)
         load_member(1, 2)
-        load_member(1, 3)
         load_prior(0, HEAD_BLOCKS, 1)
         load_prior(1, 0, BLOCKS)
 
@@ -165,7 +173,7 @@ def tile_smoothed_target_encoding_k2_kernel(
                 grouped[1, k] = ring.tile([P, W, PACK], BF16, name="grouped", align_bytes=64)
             copy(
                 out=grouped[1, k][:].rearrange("p (t m e) j -> p m t e j", t=PACK, e=2)[:, part],
-                in_=member_raw[1, k][:].rearrange("p j (m e t) -> p m t e j", e=2, t=PACK)[:, part],
+                in_=member_raw[1, k].rearrange("p j (m e t) -> p m t e j", e=2, t=PACK)[:, part],
             )
 
         def quantise_member(g, k, cols, source):
@@ -371,6 +379,10 @@ def tile_smoothed_target_encoding_k2_kernel(
                 for unit in units_of(r):
                     mx_pass(unit, k)
 
+        all_pairs, low_pairs, high_pairs = slice(0, P // 2), slice(0, P // 4), slice(P // 4, P // 2)
+        interleave_by_slot(PASSES - 1, nc.vector.tensor_copy, all_pairs)
+        quantise_member(1, PASSES - 1, slice(0, W), grouped[1, PASSES - 1])
+
         for b, blocks in ((0, HEAD_BLOCKS), (HEAD_BLOCKS, 1)):
             tile = weight_tile(0, b, blocks)
             for t in range(PACK):
@@ -378,7 +390,6 @@ def tile_smoothed_target_encoding_k2_kernel(
         direct_weight = weight_tile(1, 0, 1)
         late_weight = []
 
-        all_pairs, low_pairs, high_pairs = slice(0, P // 2), slice(0, P // 4), slice(P // 4, P // 2)
         rounded_on_scalar = []
 
         def scalar_round_half(half):
@@ -388,7 +399,7 @@ def tile_smoothed_target_encoding_k2_kernel(
         def scalar_jobs(r):
             jobs = []
             if r == MEMBER_ROUNDS[-1]:
-                jobs.append(lambda: interleave_by_slot(PASSES - 1, nc.scalar.copy, high_pairs))
+                jobs.append(lambda: interleave_by_slot(MEMBER_ROUNDS.index(r), nc.scalar.copy, high_pairs))
             if r + 3 in direct_rounds:
                 slots = [unit[2] for unit in units_of(r + 3)]
                 jobs.append(lambda: [make_weight(direct_weight, 1, 0, t) for t in slots])
@@ -438,7 +449,7 @@ def tile_smoothed_target_encoding_k2_kernel(
                 round_half(nc.vector.tensor_copy, half)
             if r in MEMBER_ROUNDS:
                 k = MEMBER_ROUNDS.index(r)
-                interleave_by_slot(k, nc.vector.tensor_copy, low_pairs if k == PASSES - 1 else all_pairs)
+                interleave_by_slot(k, nc.vector.tensor_copy, low_pairs if r == MEMBER_ROUNDS[-1] else all_pairs)
             for half in to_finish:
                 finish_half(half)
             if r in MEMBER_ROUNDS:

from contextlib import ExitStack

import concourse.mybir as mybir
from concourse.masks import make_identity

R, C, T = 2048, 1024, 1536
FLOPS = 2 * R * C * T

F32 = mybir.dt.float32
BF16 = mybir.dt.bfloat16
U32 = mybir.dt.uint32
I32 = mybir.dt.int32
U8 = mybir.dt.uint8
E4M3X4 = mybir.dt.float8_e4m3fn_x4
E5M2X4 = mybir.dt.float8_e5m2_x4
ACT = mybir.ActivationFunctionType
ALU = mybir.AluOpType

P = 128
PACK = 4
W = P * PACK
HALF = W // 2
PASSES = R // W
GROUPS = C // W
BLOCKS = T // W
STRIPS = T // P
QUADRANTS = 4

DIRECT_BLOCK = (1, 0)
HEAD_BLOCKS = 2
MEMBER_ROUNDS = (2, 4, 5)
SCALAR_LAG = 3
VECTOR_LAG = 2


def tile_smoothed_target_encoding_k2_kernel(
    tc, member, target_words, target_scales, counts, smooth, prior, out_0, out_1, out_2
):
    nc = tc.nc

    with ExitStack() as ctx:
        keep = ctx.enter_context(tc.tile_pool(name="keep", bufs=1))
        ring = ctx.enter_context(tc.tile_pool(name="ring", bufs=2))
        psum = ctx.enter_context(tc.psum_pool(name="psum", bufs=8))
        ctx.enter_context(tc.manual_schedule())

        def bank():
            return psum.tile([P, W], F32, name="bank")

        def by_slot(tensor, group, col0, width):
            rows = tensor[group * W : (group + 1) * W, col0 : col0 + width]
            return rows.rearrange("(p t) c -> p t c", t=PACK)

        smooth_rows = keep.tile([P, P], BF16, name="smooth_rows")
        nc.vector.memset(smooth_rows[:], 0.0)
        d_scales = keep.tile([P, PASSES, T], U8, name="d_scales", align_bytes=64)
        nc.vector.memset(d_scales[:].bitcast(I32), 0)

        count_bf = keep.tile([P, GROUPS, PACK], BF16, name="count_bf")
        nc.scalar.dma_start(out=count_bf[:], in_=counts.rearrange("(g p t) -> p g t", g=GROUPS, t=PACK))
        smooth_strips = smooth.rearrange("(s j) -> s j", j=P)
        nc.scalar.dma_start(out=smooth_rows[0:8, :], in_=smooth_strips[0:8, :])
        nc.scalar.dma_start(out=smooth_rows[8:STRIPS, :], in_=smooth_strips[8:STRIPS, :])

        ident_bf = keep.tile([P, P], BF16, name="ident_bf")
        make_identity(nc, ident_bf[:])
        ident_f32 = keep.tile([P, P], F32, name="ident_f32")
        make_identity(nc, ident_f32[:])

        member_raw = {}
        prior_sb = {}
        d_codes = {}
        d_words = target_words.rearrange("k p n t -> p k (n t)").bitcast(I32)

        def load_member(g, k):
            member_raw[g, k] = keep.tile([P, PACK, W], BF16, name="member_raw_%d_%d" % (g, k))[:]
            nc.sync.dma_start(out=member_raw[g, k], in_=by_slot(member, k, g * W, W))

        def load_member_both_groups(k):
            rows = keep.tile([P, PACK, C], BF16, name="member_rows_%d" % k)
            nc.sync.dma_start(out=rows[:], in_=by_slot(member, k, 0, C))
            for g in range(GROUPS):
                member_raw[g, k] = rows[:, :, g * W : (g + 1) * W]

        def load_prior(g, b0, blocks):
            tile = keep.tile([P, PACK, blocks * W], BF16, name="prior_%d_%d" % (g, b0))
            nc.sync.dma_start(out=tile[:], in_=by_slot(prior, g, b0 * W, blocks * W))
            for n in range(blocks):
                prior_sb[g, b0 + n] = tile[:, :, n * W : (n + 1) * W]

        def load_d_scales(col0, width):
            for q in range(QUADRANTS):
                rows = target_scales[:, 4 * q : 4 * q + 4, col0 : col0 + width].rearrange("k r n -> r k n")
                nc.sync.dma_start(
                    out=d_scales[32 * q : 32 * q + 4, :, col0 : col0 + width].bitcast(I32), in_=rows.bitcast(I32)
                )

        def load_d_head(k):
            words = keep.tile([P, HEAD_BLOCKS * W], U32, name="d_head_%d" % k, align_bytes=64)
            nc.sync.dma_start(out=words[:].bitcast(I32), in_=d_words[:, k, 0 : HEAD_BLOCKS * W])
            for b in range(HEAD_BLOCKS):
                d_codes[k, b] = words[:, b * W : (b + 1) * W]

        def load_d_block(b):
            words = keep.tile([P, PASSES, W], U32, name="d_block_%d" % b, align_bytes=64)
            nc.sync.dma_start(out=words[:].bitcast(I32), in_=d_words[:, :, b * W : (b + 1) * W])
            for k in range(PASSES):
                d_codes[k, b] = words[:, k, :]

        for k in range(PASSES):
            if k < PASSES - 1:
                load_member(0, k)
            else:
                load_member_both_groups(k)
            if k == 0:
                load_d_scales(0, HEAD_BLOCKS * W)
            load_d_head(k)
        load_prior(0, 0, HEAD_BLOCKS)
        load_member(1, 0)
        load_d_scales(HEAD_BLOCKS * W, W)
        load_d_block(HEAD_BLOCKS)
        load_member(1, 1)
        load_member(1, 2)
        load_prior(0, HEAD_BLOCKS, 1)
        load_prior(1, 0, BLOCKS)

        spread = [bank() for b in range(BLOCKS)]
        for s in range(STRIPS):
            nc.tensor.matmul(
                out=spread[s // PACK][:, (s % PACK) * P : (s % PACK + 1) * P],
                lhsT=ident_bf[:, s : s + 1].to_broadcast([P, P]),
                rhs=smooth_rows[:],
                start=True,
                stop=True,
            )
        smooth_cols = bank()
        nc.tensor.matmul(
            out=smooth_cols[:, 0:STRIPS], lhsT=smooth_rows[:], rhs=ident_bf[:, 0:STRIPS], start=True, stop=True
        )
        count_cols = count_bf[:].rearrange("p g t -> p (g t)")
        ln_count = keep.tile([P, GROUPS * PACK], F32, name="ln_count")
        nc.scalar.activation(out=ln_count[:], in_=count_cols, func=ACT.Ln)
        ln_smooth = keep.tile([P, T], F32, name="ln_smooth")
        for b in range(BLOCKS):
            nc.scalar.activation(out=ln_smooth[:, b * W : (b + 1) * W], in_=spread[b][:], func=ACT.Ln)
        neg_ln_count = keep.tile([P, GROUPS * PACK], F32, name="neg_ln_count")
        inv_count = keep.tile([P, GROUPS * PACK], F32, name="inv_count")
        inv_smooth = keep.tile([P, STRIPS], F32, name="inv_smooth")

        def small_vector_work():
            nc.vector.tensor_scalar(out=neg_ln_count[:], in0=ln_count[:], scalar1=-1.0, scalar2=None, op0=ALU.mult)
            nc.vector.reciprocal(out=inv_smooth[:], in_=smooth_cols[:, 0:STRIPS])
            nc.vector.reciprocal(out=inv_count[:], in_=count_cols)

        grouped = {}
        member_codes = {}
        member_scales = {}
        for g in range(GROUPS):
            for k in range(PASSES):
                member_codes[g, k] = keep.tile([P, W], U32, name="member_codes_%d_%d" % (g, k), align_bytes=64)
                member_scales[g, k] = keep.tile([P, W], U8, name="member_scales_%d_%d" % (g, k), align_bytes=64)

        def interleave_in_order(k, h):
            grouped[0, k, h] = ring.tile([P, HALF, PACK], BF16, name="grouped_half", align_bytes=64)
            raw = member_raw[0, k][:, :, h * HALF : (h + 1) * HALF]
            nc.vector.tensor_copy(
                out=grouped[0, k, h][:].rearrange("p (c i) j -> p c j i", i=4),
                in_=raw.rearrange("p j (c i) -> p c j i", i=4),
            )

        def interleave_by_slot(k, copy, part):
            if (1, k) not in grouped:
                grouped[1, k] = ring.tile([P, W, PACK], BF16, name="grouped", align_bytes=64)
            copy(
                out=grouped[1, k][:].rearrange("p (t m e) j -> p m t e j", t=PACK, e=2)[:, part],
                in_=member_raw[1, k].rearrange("p j (m e t) -> p m t e j", e=2, t=PACK)[:, part],
            )

        def quantise_member(g, k, cols, source):
            nc.vector.quantize_mx(
                out=member_codes[g, k][:, cols].bitcast(E4M3X4),
                scales=member_scales[g, k][:, cols],
                in_=source[:].rearrange("p c j -> p (c j)"),
            )

        weight = {}

        def weight_tile(g, b, blocks):
            tile = ring.tile([P, PACK, blocks * W], F32, name="weight_%d" % blocks, bufs=2 // blocks)
            for n in range(blocks):
                weight[g, b + n] = tile[:, :, n * W : (n + 1) * W]
            return tile

        def make_weight(tile, g, b, t):
            col = g * PACK + t
            direct = (g, b) == DIRECT_BLOCK
            nc.scalar.activation(
                out=tile[:, t, :],
                in_=ln_smooth[:, b * W : b * W + tile.shape[2]],
                func=ACT.Sigmoid,
                bias=(ln_count if direct else neg_ln_count)[:, col : col + 1],
                scale=-1.0 if direct else 1.0,
            )

        sums = {}
        scaled = {}
        joined = {}
        shrunk_prior = {}
        y_block = {}
        y_tile = {}
        y_bf = {}
        y_codes = [keep.tile([P, T], U32, name="y_codes_%d" % g, align_bytes=64) for g in range(GROUPS)]
        y_scales = [keep.tile([P, T], U8, name="y_scales_%d" % g, align_bytes=64) for g in range(GROUPS)]

        def mx_pass(unit, k):
            g, b, i = unit
            if k == 0:
                sums[unit] = bank()
            strip = slice(i * P, (i + 1) * P)
            m_words, m_scales = member_codes[g, k], member_scales[g, k]
            d_block_scales = d_scales[:, k, b * W : (b + 1) * W]
            if (g, b) == DIRECT_BLOCK:
                lhs, lhs_scale = m_words[:, strip].bitcast(E4M3X4), m_scales[:, strip]
                rhs, rhs_scale = d_codes[k, b].bitcast(E5M2X4), d_block_scales
            else:
                lhs, lhs_scale = d_codes[k, b][:, strip].bitcast(E5M2X4), d_block_scales[:, strip]
                rhs, rhs_scale = m_words[:].bitcast(E4M3X4), m_scales[:]
            nc.tensor.matmul_mx(
                out=sums[unit][:],
                lhsT=lhs,
                lhsT_scale=lhs_scale,
                rhs=rhs,
                rhs_scale=rhs_scale,
                start=(k == 0),
                stop=(k == PASSES - 1),
            )

        def scale_out(unit):
            g, b, i = unit
            scaled[unit] = ring.tile([P, PACK, P], F32, name="scaled", bufs=6)
            order = "p (m t) -> p t m" if g == 0 else "p (t m) -> p t m"
            strip = b * PACK + i
            nc.scalar.activation(
                out=scaled[unit][:],
                in_=sums[unit][:].rearrange(order, t=PACK),
                func=ACT.Copy,
                scale=inv_smooth[:, strip : strip + 1],
            )

        def turn_and_add(units):
            for unit in units:
                g, b, i = unit
                joined[unit] = bank()
                nc.tensor.matmul(
                    out=joined[unit][:].rearrange("p (t j) -> p t j", t=PACK),
                    lhsT=ident_bf[:],
                    rhs=prior_sb[g, b][:, :, i * P : (i + 1) * P],
                    start=True,
                    stop=False,
                )
            for unit in units:
                for t in range(PACK):
                    nc.tensor.matmul(
                        out=joined[unit][:, t * P : (t + 1) * P],
                        lhsT=scaled[unit][:, t, :],
                        rhs=ident_f32[:],
                        is_transpose=True,
                        start=False,
                        stop=(t == PACK - 1),
                    )

        def weigh_joined(unit):
            g, b, i = unit
            if i == 0:
                y_block[g, b] = ring.tile([P, PACK, W], F32, name="y_turned", bufs=3)
                for h in range(2):
                    y_tile[g, b, h] = y_block[g, b][:, :, h * HALF : (h + 1) * HALF]
            nc.vector.tensor_tensor(
                out=y_tile[g, b, i // 2][:, :, (i % 2) * P : (i % 2 + 1) * P],
                in0=joined[unit][:].rearrange("p (t j) -> p t j", t=PACK),
                in1=weight[g, b][:, :, i * P : (i + 1) * P],
                op=ALU.mult,
            )

        y_direct = keep.tile([P, PACK, W], F32, name="y_direct")
        for h in range(2):
            y_tile[DIRECT_BLOCK + (h,)] = y_direct[:, :, h * HALF : (h + 1) * HALF]

        def weigh_sums(unit):
            g, b, t = unit
            nc.vector.scalar_tensor_tensor(
                out=y_direct[:, t, :],
                in0=sums[unit][:],
                scalar=inv_count[:, g * PACK + t : g * PACK + t + 1],
                in1=weight[g, b][:, t, :],
                op0=ALU.mult,
                op1=ALU.mult,
            )

        def shrink_prior(unit):
            g, b, t = unit
            shrunk_prior[unit] = ring.tile([P, W], F32, name="shrunk_prior")
            nc.vector.scalar_tensor_tensor(
                out=shrunk_prior[unit][:],
                in0=weight[g, b][:, t, :],
                scalar=1.0,
                in1=prior_sb[g, b][:, t, :],
                op0=ALU.subtract,
                op1=ALU.mult,
            )

        def join_prior(unit):
            row = y_direct[:, unit[2], :]
            nc.vector.tensor_tensor(out=row, in0=row, in1=shrunk_prior[unit][:], op=ALU.subtract)

        def round_y(copy, g, col0, source):
            width = source.shape[2]
            y_bf[g, col0] = ring.tile([P, HALF, PACK], BF16, name="y_bf", bufs=5, align_bytes=64)[:, 0:width, :]
            copy(
                out=y_bf[g, col0].rearrange("p (c i) t -> p c t i", i=4),
                in_=source.rearrange("p t (c i) -> p c t i", i=4),
            )

        def quantise_y(g, col0):
            width = y_bf[g, col0].shape[1]
            nc.vector.quantize_mx(
                out=y_codes[g][:, col0 : col0 + width].bitcast(E4M3X4),
                scales=y_scales[g][:, col0 : col0 + width],
                in_=y_bf[g, col0].rearrange("p c t -> p (c t)"),
            )

        def store_y(g, col0, source):
            nc.sync.dma_start(out=by_slot(out_0, g, col0, source.shape[2]), in_=source)

        def store_codes(g, col0, width):
            words = out_1[g].rearrange("p m t -> p (m t)").bitcast(I32)
            nc.sync.dma_start(out=words[:, col0 : col0 + width], in_=y_codes[g][:, col0 : col0 + width].bitcast(I32))

        def store_scales(g, col0, width, queues):
            for q in range(QUADRANTS):
                queues[q % len(queues)].dma_start(
                    out=out_2[g, 4 * q : 4 * q + 4, col0 : col0 + width].bitcast(I32),
                    in_=y_scales[g][32 * q : 32 * q + 4, col0 : col0 + width].bitcast(I32),
                )

        def first_col(half):
            return half[1] * W + half[2] * HALF

        def round_half(copy, half):
            round_y(copy, half[0], first_col(half), y_tile[half])

        def finish_half(half):
            g, b, h = half
            quantise_y(g, first_col(half))
            if h == 1:
                store_codes(g, b * W, W)
            if half == (0, BLOCKS - 1, 1):
                store_scales(0, 0, T, [nc.sync])
            if half == (1, BLOCKS - 2, 1):
                store_scales(1, 0, T - W, [nc.sync])

        rounds = [(g, b, h) for g in range(GROUPS) for b in range(BLOCKS) for h in range(2)]
        last = len(rounds) - 1
        head_rounds = 2 * HEAD_BLOCKS
        direct_rounds = [r for r in range(len(rounds)) if rounds[r][:2] == DIRECT_BLOCK]

        def units_of(r):
            g, b, h = rounds[r]
            return [(g, b, 2 * h), (g, b, 2 * h + 1)]

        for k in range(PASSES):
            for h in range(2):
                interleave_in_order(k, h)
            for h in range(2):
                quantise_member(0, k, slice(h * HALF, (h + 1) * HALF), grouped[0, k, h])
            if k == 0:
                small_vector_work()
            for r in range(head_rounds):
                for unit in units_of(r):
                    mx_pass(unit, k)

        all_pairs, low_pairs, high_pairs = slice(0, P // 2), slice(0, P // 4), slice(P // 4, P // 2)
        interleave_by_slot(PASSES - 1, nc.vector.tensor_copy, all_pairs)
        quantise_member(1, PASSES - 1, slice(0, W), grouped[1, PASSES - 1])

        for b, blocks in ((0, HEAD_BLOCKS), (HEAD_BLOCKS, 1)):
            tile = weight_tile(0, b, blocks)
            for t in range(PACK):
                make_weight(tile, 0, b, t)
        direct_weight = weight_tile(1, 0, 1)
        late_weight = []

        rounded_on_scalar = []

        def scalar_round_half(half):
            round_half(nc.scalar.copy, half)
            rounded_on_scalar.append(half)

        def scalar_jobs(r):
            jobs = []
            if r == MEMBER_ROUNDS[-1]:
                jobs.append(lambda: interleave_by_slot(MEMBER_ROUNDS.index(r), nc.scalar.copy, high_pairs))
            if r + 3 in direct_rounds:
                slots = [unit[2] for unit in units_of(r + 3)]
                jobs.append(lambda: [make_weight(direct_weight, 1, 0, t) for t in slots])
            if r in direct_rounds:
                if not late_weight:
                    late_weight.append(weight_tile(1, 1, 2))
                for unit in units_of(r):
                    jobs.append(lambda t=unit[2]: make_weight(late_weight[0], 1, 1, t))
            if 0 <= r - SCALAR_LAG < direct_rounds[0]:
                jobs.append(lambda: scalar_round_half(rounds[r - SCALAR_LAG]))
            if r - VECTOR_LAG == direct_rounds[-1]:
                jobs.append(lambda: scalar_round_half(DIRECT_BLOCK + (1,)))
            return jobs

        def vector_half(r):
            done = r - VECTOR_LAG
            if done == direct_rounds[-1]:
                return [DIRECT_BLOCK + (0,)]
            return [rounds[done]] if done > direct_rounds[-1] else []

        for r in range(len(rounds)):
            units = units_of(r)
            direct = r in direct_rounds
            before = units_of(r - 1) if r > 0 and r - 1 not in direct_rounds else []
            passes = range(PASSES if r < head_rounds else 0, PASSES)
            early, late = (units[:1], units[1:]) if r == last else (units, [])
            for unit in early:
                for k in passes:
                    mx_pass(unit, k)

            to_finish = list(rounded_on_scalar)
            rounded_on_scalar.clear()
            jobs = scalar_jobs(r)
            for n in range(max(len(jobs), len(early))):
                for job in jobs[n : n + 1]:
                    job()
                if not direct and n < len(early):
                    scale_out(early[n])

            turn_and_add(before)
            for unit in late:
                for k in passes:
                    mx_pass(unit, k)
                scale_out(unit)

            for half in vector_half(r):
                round_half(nc.vector.tensor_copy, half)
            if r in MEMBER_ROUNDS:
                k = MEMBER_ROUNDS.index(r)
                interleave_by_slot(k, nc.vector.tensor_copy, low_pairs if r == MEMBER_ROUNDS[-1] else all_pairs)
            for half in to_finish:
                finish_half(half)
            if r in MEMBER_ROUNDS:
                quantise_member(1, k, slice(0, W), grouped[1, k])
            for half in vector_half(r):
                finish_half(half)
            if direct:
                for unit in units:
                    weigh_sums(unit)
            for unit in before:
                weigh_joined(unit)
            if before and rounds[r - 1][0] == GROUPS - 1:
                store_y(rounds[r - 1][0], first_col(rounds[r - 1]), y_tile[rounds[r - 1]])
            elif before and rounds[r - 1][2] == 1:
                g, b, h = rounds[r - 1]
                store_y(g, b * W, y_block[g, b][:])
            if direct:
                for unit in units:
                    shrink_prior(unit)
                for unit in units:
                    join_prior(unit)
                slots = slice(units[0][2], units[1][2] + 1)
                nc.sync.dma_start(
                    out=by_slot(out_0, DIRECT_BLOCK[0], DIRECT_BLOCK[1] * W, W)[:, slots, :], in_=y_direct[:, slots, :]
                )

        g = GROUPS - 1
        turn_and_add(units_of(last))
        round_half(nc.vector.tensor_copy, rounds[last - 1])
        first, second = units_of(last)
        col0 = first_col(rounds[last])
        weigh_joined(first)
        quantise_y(g, col0 - HALF)
        store_codes(g, col0 - HALF, HALF)
        y_last = y_tile[rounds[last]]
        weigh_joined(second)
        store_y(g, col0, y_last)
        round_y(nc.scalar.copy, g, col0, y_last[:, :, 0:P])
        round_y(nc.vector.tensor_copy, g, col0 + P, y_last[:, :, P:HALF])
        quantise_y(g, col0)
        quantise_y(g, col0 + P)
        store_codes(g, col0, HALF)
        store_scales(g, T - W, W, [nc.scalar, nc.sync])
